import numpy as np
import ml_dtypes


def mxq(x, axis, fmt="e4m3"):
    dtype, down = {"e4m3": (ml_dtypes.float8_e4m3fn, 7), "e5m2": (ml_dtypes.float8_e5m2, 14)}[fmt]
    v = np.moveaxis(np.asarray(x, np.float32).astype(ml_dtypes.bfloat16).astype(np.float64), axis, -1)
    blocks = v.reshape(v.shape[:-1] + (-1, 32))
    amax = np.abs(blocks).max(-1, keepdims=True)
    byte = np.maximum(np.where(amax > 0, np.frexp(amax)[1] - 1 + 127, 0) - down, 1)
    scale = np.exp2(byte - 127.0)
    codes = (blocks / scale).astype(np.float32).astype(dtype).astype(np.float64)
    return np.moveaxis((codes * scale).reshape(v.shape), -1, axis)


WIDE = False


def mx_kscale(k):
    if not WIDE:
        return np.ones(k)
    levels = np.array([10, -10, 5, -5, 0])
    if k % 512:
        return np.exp2(np.random.permutation(np.resize(levels, k // 32))).repeat(32)
    a = np.empty((k // 512, 16))
    for p in range(k // 512):
        a[p, :8] = np.random.permutation(np.resize(levels, 8))
        for g in range(8):
            far = levels[np.abs(levels - a[p, g]) >= 10]
            a[p, g + 8] = far[np.random.randint(len(far))]
    return np.exp2(a.ravel()).repeat(32)


BF16 = ml_dtypes.bfloat16


def bf(x):
    return np.asarray(x, np.float32).astype(BF16)


def f64(x):
    return np.asarray(x).astype(np.float64)

E4M3FN = np.array([(-1.0 if i & 128 else 1.0) * ((1.0 + (i & 7) / 8.0) * 2.0 ** (((i >> 3) & 15) - 7) if i & 120 else (i & 7) * 2.0 ** -9) for i in range(256)])


def e4m3fn_bytes(y):
    return np.clip(np.asarray(y, np.float64), -448.0, 448.0).astype(np.float32).astype(ml_dtypes.float8_e4m3fn).view(np.uint8)


def e4m3fn_values(b):
    return E4M3FN[b]


P, C, H, Q = 1024, 512, 2048, 128


def setup_inputs():
    s, t = mx_kscale(C), mx_kscale(H)
    w1 = np.random.standard_normal((C, H)) / np.sqrt(C) / s[:, None]
    w2 = np.random.standard_normal((C, H)) / np.sqrt(H) / t
    w1_scale = (np.abs(w1).reshape(C // Q, Q, H // Q, Q).max(axis=(1, 3)) / 448.0).astype(np.float32)
    w2_scale = (np.abs(w2).reshape(C // Q, Q, H // Q, Q).max(axis=(1, 3)) / 448.0).astype(np.float32)
    return {"y": bf(np.random.standard_normal((P, C)) * s),
            "w1_bytes": e4m3fn_bytes(w1 / np.repeat(np.repeat(f64(w1_scale), Q, axis=0), Q, axis=1)),
            "w1_scale": w1_scale,
            "g": bf((1 + 0.1 * np.random.standard_normal(H)) * t),
            "w2_bytes": e4m3fn_bytes(w2 / np.repeat(np.repeat(f64(w2_scale), Q, axis=0), Q, axis=1)),
            "w2_scale": w2_scale,
            "gamma": bf(1 + 0.1 * np.random.standard_normal(C)),
            "r": bf(np.random.standard_normal((C, P)))}


def reference(y, w1_bytes, w1_scale, g, w2_bytes, w2_scale, gamma, r):
    w1 = e4m3fn_values(w1_bytes) * np.repeat(np.repeat(f64(w1_scale), Q, axis=0), Q, axis=1)
    w2 = e4m3fn_values(w2_bytes) * np.repeat(np.repeat(f64(w2_scale), Q, axis=0), Q, axis=1)
    z = mxq(f64(y), 1, "e4m3") @ mxq(w1, 0, "e4m3")
    a = 0.5 * z * (1 + np.tanh(np.sqrt(2 / np.pi) * (z + 0.044715 * z * z * z)))
    h = a * f64(g)
    o = mxq(w2, 1, "e4m3") @ mxq(h, 1, "e4m3").T
    return f64(r) + f64(gamma)[:, None] * o

@@ -1,0 +1,291 @@
+from contextlib import ExitStack
+
+import concourse.mybir as mybir
+from concourse.masks import make_identity
+
+F32 = mybir.dt.float32
+BF16 = mybir.dt.bfloat16
+U32 = mybir.dt.uint32
+U8 = mybir.dt.uint8
+FP8 = mybir.dt.float8_e4m3fn
+FP8X4 = mybir.dt.float8_e4m3fn_x4
+MULT = mybir.AluOpType.mult
+ADD = mybir.AluOpType.add
+GELU = mybir.ActivationFunctionType.Gelu_apprx_tanh
+COPY = mybir.ActivationFunctionType.Copy
+
+P = 128
+NPOS, C, H = 1024, 512, 2048
+NG = H // 512
+NI = C // P
+FLOPS = 2 * NPOS * C * H * 2
+
+PLAN = {'w1w': {1: ('v', -1), 2: ('v', 0), 3: ('s', 7)}, 'w1i': {1: (-1, -1, -1, -1), 2: (1, 2, 6, 8), 3: (9, 9, 9, 14)}, 'w2w': {0: ('s', 0), 1: ('v', 0), 2: ('v', -1), 3: ('s', 12)}, 'turn': (7, 7, 9, 12, 14, 15, 16, 16), 'ex': (('s', 2), ('s', 3), ('v', 1), ('s', 2), ('v', 0), ('s', 0), ('s', 2), ('s', 3)), 's2': (21, 26, 28), 'fin0': (29, 29, 30, 32), 's2b': 30, 'w10': 'vs'}
+
+
+def tile_convnext_pointwise_pair_d7_kernel(
+    tc, y, w1_bytes, w1_scale, g, w2_bytes, w2_scale, gamma, r, out
+):
+    nc = tc.nc
+    with ExitStack() as ctx:
+        keep = ctx.enter_context(tc.tile_pool(name="keep", bufs=1))
+        gelp = ctx.enter_context(tc.tile_pool(name="gelp", bufs=12))
+        hp = ctx.enter_context(tc.tile_pool(name="hp", bufs=3))
+        op = ctx.enter_context(tc.tile_pool(name="op", bufs=1))
+        psum = ctx.enter_context(tc.psum_pool(name="psum", bufs=1))
+        ctx.enter_context(tc.manual_schedule())
+
+        def sb(shape, dt, name):
+            return keep.tile(shape, dt, name=name, align_bytes=64)
+
+        ident = sb([P, P], F32, "ident")
+        w1s = sb([P, 16], F32, "w1s")
+        w2s_all = sb([P, 4, 16], F32, "w2s_all")
+        w2s = sb([P, 4, 4], F32, "w2s")
+        g_sb = sb([P, 16], BF16, "g_sb")
+        gamma_sb = sb([P, 4, 2], BF16, "gamma_sb")
+        y_sb = [sb([P, 2, C], BF16, "y_sb%d" % p) for p in range(4)]
+        y_grp = [sb([P, 1024], BF16, "y_grp%d" % p) for p in range(4)]
+        y_codes = sb([P, NPOS], U32, "y_codes")
+        y_scl = sb([P, NPOS], U8, "y_scl")
+        w1_raw = [sb([P, 2048], U8, "w1_raw%d" % k) for k in range(NG)]
+        w1_wide = [sb([P, 2048], BF16, "w1_wide%d" % k) for k in range(NG)]
+        w1_grp = [sb([P, 2048], BF16, "w1_grp%d" % k) for k in range(NG)]
+        w1_codes = [sb([P, 512], U32, "w1_codes%d" % k) for k in range(NG)]
+        w1_scl = [sb([P, 512], U8, "w1_scl%d" % k) for k in range(NG)]
+        w2_raw = [sb([P, 2048], U8, "w2_raw%d" % i) for i in range(NI)]
+        w2_wide = [sb([P, 2048], BF16, "w2_wide%d" % i) for i in range(NI)]
+        w2_grp = [sb([P, 2048], BF16, "w2_grp%d" % k) for k in range(NG)]
+        w2_codes = [sb([P, 512], U32, "w2_codes%d" % k) for k in range(NG)]
+        w2_scl = [sb([P, 512], U8, "w2_scl%d" % k) for k in range(NG)]
+        h_codes = [[sb([P, 512], U32, "h_codes%d_%d" % (k, n)) for n in range(2)] for k in range(NG)]
+        h_scl = [[sb([P, 512], U8, "h_scl%d_%d" % (k, n)) for n in range(2)] for k in range(NG)]
+        r_sb = sb([P, NI, NPOS], BF16, "r_sb")
+
+        gel = {}
+        hbf = {}
+        acc = {}
+        tb = {}
+
+        def load_w1(k):
+            src = w1_bytes.rearrange("(p t) n -> p t n", t=4)[:, :, 512 * k : 512 * (k + 1)]
+            nc.sync.dma_start(out=w1_raw[k][:].rearrange("p (t n) -> p t n", t=4), in_=src)
+
+        def load_y(p):
+            nc.sync.dma_start(
+                out=y_sb[p][:], in_=y[256 * p : 256 * (p + 1), :].rearrange("(a p) k -> p a k", p=P)
+            )
+
+        def load_w2(i):
+            nc.sync.dma_start(out=w2_raw[i][:], in_=w2_bytes[P * i : P * (i + 1), :])
+
+        def widen(eng, dst, src, lo, hi):
+            d, s = dst[:, lo:hi], src[:, lo:hi].bitcast(FP8)
+            if eng == "s":
+                nc.scalar.copy(out=d, in_=s)
+            else:
+                nc.vector.tensor_copy(out=d, in_=s)
+
+        def interleave_w1(k, jb):
+            o = w1_grp[k][:].rearrange("p (t m j) -> p m j t", t=4, j=4)[:, 32 * jb : 32 * (jb + 1)]
+            i = w1_wide[k][:].rearrange("p (j m t) -> p m j t", j=4, t=4)[:, 32 * jb : 32 * (jb + 1)]
+            nc.vector.tensor_scalar(
+                out=o, in0=i, scalar1=w1s[:, 4 * k + jb : 4 * k + jb + 1], scalar2=None, op0=MULT
+            )
+
+        def quant_w1(k):
+            nc.vector.quantize_mx(out=w1_codes[k][:].bitcast(FP8X4), scales=w1_scl[k][:], in_=w1_grp[k][:])
+
+        def turn_y(p):
+            t = psum.tile([P, 2, 2, P], F32, name="a%d" % p)
+            words = y_sb[p][:].rearrange("p a k -> p (a k)").bitcast(F32)
+            for a in range(2):
+                for u in range(2):
+                    nc.tensor.transpose(t[:, a, u, :], words[:, 256 * a + u : 256 * (a + 1) : 2], ident[:])
+            return t
+
+        def exit_y(eng, p, t):
+            o = y_grp[p][:].bitcast(F32).rearrange("p (a r u) -> p a r u", a=2, u=2)
+            i = t[:].rearrange("p a u r -> p a r u")
+            if eng == "s":
+                nc.scalar.copy(out=o, in_=i)
+            else:
+                nc.vector.tensor_copy(out=o, in_=i)
+
+        def quant_y(p):
+            cols = slice(256 * p, 256 * (p + 1))
+            nc.vector.quantize_mx(out=y_codes[:, cols].bitcast(FP8X4), scales=y_scl[:, cols], in_=y_grp[p][:])
+
+        def z_unit(u):
+            k, b = divmod(u, 8)
+            z = psum.tile([P, 4, P], F32, name="z%d" % (u % 4))
+            for t in range(4):
+                nc.tensor.matmul_mx(
+                    out=z[:, t, :],
+                    lhsT=w1_codes[k][:, P * t : P * (t + 1)].bitcast(FP8X4),
+                    lhsT_scale=w1_scl[k][:, P * t : P * (t + 1)],
+                    rhs=y_codes[:, P * b : P * (b + 1)].bitcast(FP8X4),
+                    rhs_scale=y_scl[:, P * b : P * (b + 1)],
+                    start=True,
+                    stop=True,
+                )
+            return z
+
+        def gelu(u, z):
+            a = gelp.tile([P, P, 4], F32, name="gel")
+            nc.scalar.activation(out=a[:], in_=z[:].rearrange("p t n -> p n t"), func=GELU)
+            gel[u] = a
+
+        def gain(u):
+            k = u // 8
+            if u % 2 == 0:
+                hb = hp.tile([P, 1024], BF16, name="hbf", align_bytes=64)
+                hbf[u // 2] = hb
+            o = hbf[u // 2][:, 512 * (u % 2) : 512 * (u % 2 + 1)].rearrange("p (n t) -> p n t", t=4)
+            gk = g_sb[:, 4 * k : 4 * (k + 1)].unsqueeze(1).to_broadcast([P, P, 4])
+            nc.vector.tensor_tensor(out=o, in0=gel[u][:], in1=gk, op=MULT)
+
+        def quant_h(pair):
+            k, q = divmod(pair, 4)
+            n, c = divmod(q, 2)
+            cols = slice(256 * c, 256 * (c + 1))
+            nc.vector.quantize_mx(
+                out=h_codes[k][n][:, cols].bitcast(FP8X4), scales=h_scl[k][n][:, cols], in_=hbf[pair][:]
+            )
+
+        def turn_w2(ip, k, bank):
+            t = psum.tile([P, 2, 2, P], F32, name="a%d" % bank)
+            for ii in range(2):
+                words = w2_wide[2 * ip + ii][:].bitcast(F32)
+                for u in range(2):
+                    nc.tensor.transpose(t[:, ii, u, :], words[:, 256 * k + u : 256 * (k + 1) : 2], ident[:])
+            tb[ip, k] = t
+
+        def exit_w2(eng, i, k):
+            o = w2_grp[k][:, 512 * i : 512 * (i + 1)].rearrange("p (r u e) -> p r u e", u=2, e=2)
+            s = tb[i // 2, k][:, i % 2].rearrange("p u r -> p (u r)").bitcast(BF16)
+            s = s.rearrange("p (u r e) -> p r u e", u=2, e=2)
+            col = w2s[:, i, k : k + 1]
+            if eng == "s":
+                nc.scalar.activation(out=o, in_=s, func=COPY, scale=col)
+            else:
+                nc.vector.tensor_scalar(out=o, in0=s, scalar1=col, scalar2=None, op0=MULT)
+
+        def quant_w2(k):
+            nc.vector.quantize_mx(out=w2_codes[k][:].bitcast(FP8X4), scales=w2_scl[k][:], in_=w2_grp[k][:])
+
+        def stage2(n, i, k):
+            if k == 0:
+                acc[n, i] = psum.tile([P, 512], F32, name=("z%d" if n else "a%d") % i)
+            nc.tensor.matmul_mx(
+                out=acc[n, i][:],
+                lhsT=w2_codes[k][:, P * i : P * (i + 1)].bitcast(FP8X4),
+                lhsT_scale=w2_scl[k][:, P * i : P * (i + 1)],
+                rhs=h_codes[k][n][:].bitcast(FP8X4),
+                rhs_scale=h_scl[k][n][:],
+                start=(k == 0),
+                stop=(k == NG - 1),
+            )
+
+        def finish(n, i):
+            o = op.tile([P, 512], F32, name="o%d_%d" % (n, i))
+            cols = slice(512 * n, 512 * (n + 1))
+            nc.vector.scalar_tensor_tensor(
+                out=o[:], in0=acc[n, i][:], scalar=gamma_sb[:, i, 0:1], in1=r_sb[:, i, cols], op0=MULT, op1=ADD
+            )
+            nc.sync.dma_start(out=out[P * i : P * (i + 1), cols], in_=o[:])
+
+        load_w1(0)
+        for q in range(4):
+            nc.scalar.dma_start(out=w1s[32 * q : 32 * (q + 1), :], in_=w1_scale[q].partition_broadcast(32))
+        for p in range(4):
+            load_y(p)
+        load_w1(1)
+        load_w2(0)
+        load_w2(1)
+        load_w1(2)
+        load_w2(2)
+        load_w2(3)
+        load_w1(3)
+        nc.gpsimd.dma_start(out=w2s_all[:], in_=w2_scale.partition_broadcast(P))
+        nc.gpsimd.dma_start(out=g_sb[:].rearrange("p (k t) -> p k t", t=4), in_=g.rearrange("(k p t) -> p k t", p=P, t=4))
+        make_identity(nc, ident[:])
+        for q in range(4):
+            nc.gpsimd.tensor_copy(
+                out=w2s[32 * q : 32 * (q + 1)],
+                in_=w2s_all[32 * q : 32 * (q + 1)].rearrange("p i (k q) -> p i k q", q=4)[:, :, :, q],
+            )
+        nc.sync.dma_start(out=r_sb[:], in_=r.rearrange("(i p) n -> p i n", p=P))
+        nc.gpsimd.dma_start(out=gamma_sb[:, :, 0:1], in_=gamma.rearrange("(i p) -> p i", p=P).unsqueeze(2))
+
+        widen(PLAN["w10"][0], w1_wide[0], w1_raw[0], 0, 1024)
+        widen(PLAN["w10"][1], w1_wide[0], w1_raw[0], 1024, 2048)
+        for jb in range(4):
+            interleave_w1(0, jb)
+        ty = [turn_y(p) for p in range(4)]
+        exit_y("s", 0, ty[0])
+        exit_y("s", 1, ty[1])
+        quant_y(0)
+        quant_w1(0)
+        quant_y(1)
+        z = {}
+        for u in range(3):
+            z[u] = z_unit(u)
+
+        after = {u: [] for u in range(-1, 33)}
+
+        def put(u, fn, *args):
+            after[u].append((fn, args))
+
+        for k in (1, 2, 3):
+            e, s0 = PLAN["w1w"][k]
+            put(s0, widen, e, w1_wide[k], w1_raw[k], 0, 2048)
+        put(-1, exit_y, "s", 2, ty[2])
+        put(-1, exit_y, "s", 3, ty[3])
+        put(-1, quant_y, 2)
+        put(-1, quant_y, 3)
+        for k in (1, 2, 3):
+            for jb in range(4):
+                put(PLAN["w1i"][k][jb], interleave_w1, k, jb)
+            put(PLAN["w1i"][k][3] + 1, quant_w1, k)
+        for i in range(4):
+            e, s0 = PLAN["w2w"][i]
+            put(s0, widen, e, w2_wide[i], w2_raw[i], 0, 2048)
+        order = [(0, k) for k in range(4)] + [(1, k) for k in range(4)]
+        for s, (ip, k) in enumerate(order):
+            u = PLAN["turn"][s]
+            put(u, turn_w2, ip, k, s % 4)
+            e, lag = PLAN["ex"][s]
+            put(u + lag, exit_w2, e, 2 * ip, k)
+            put(u + lag, exit_w2, e, 2 * ip + 1, k)
+            if ip == 1:
+                put(u + lag + 1, quant_w2, k)
+        for k in range(3):
+            for i in range(4):
+                put(PLAN["s2"][k], stage2, 0, i, k)
+        for i in range(4):
+            put(28, stage2, 0, i, 3)
+        for i in range(4):
+            put(PLAN["fin0"][i], finish, 0, i)
+        for k in range(3):
+            for i in range(4):
+                put(PLAN["s2b"] + k, stage2, 1, i, k)
+
+        for fn, args in after[-1]:
+            fn(*args)
+        for u in range(32):
+            if u + 3 < 32:
+                z[u + 3] = z_unit(u + 3)
+            gelu(u, z[u])
+            gain(u)
+            if u % 2 == 0 and u:
+                quant_h(u // 2 - 1)
+            for fn, args in after[u]:
+                fn(*args)
+        quant_h(15)
+        for fn, args in after[32]:
+            fn(*args)
+        for i in range(4):
+            stage2(1, i, 3)
+        for i in range(4):
+            finish(1, i)

@@ -20,7 +20,17 @@ NG = H // 512
 NI = C // P
 FLOPS = 2 * NPOS * C * H * 2
 
-PLAN = {'w1w': {1: ('v', -1), 2: ('v', 0), 3: ('s', 7)}, 'w1i': {1: (-1, -1, -1, -1), 2: (1, 2, 6, 8), 3: (9, 9, 9, 14)}, 'w2w': {0: ('s', 0), 1: ('v', 0), 2: ('v', -1), 3: ('s', 12)}, 'turn': (7, 7, 9, 12, 14, 15, 16, 16), 'ex': (('s', 2), ('s', 3), ('v', 1), ('s', 2), ('v', 0), ('s', 0), ('s', 2), ('s', 3)), 's2': (21, 26, 28), 'fin0': (29, 29, 30, 32), 's2b': 30, 'w10': 'vs'}
+RING = 6
+AHEAD = 4
+Y_AT = 1
+LAG = 2
+IL_FIRST = 2
+W2_FIRST = 2
+W2_PERIOD = 6
+VEC_EXITS = (1, 3)
+
+CHUNKS = ((0, 4), (4, 2), (6, 1), (7, 1))
+UNITS = [(k, b0 + b) for b0, nb in CHUNKS for k in range(NG) for b in range(nb)]
 
 
 def tile_convnext_pointwise_pair_d7_kernel(
@@ -29,10 +39,10 @@ def tile_convnext_pointwise_pair_d7_kernel(
     nc = tc.nc
     with ExitStack() as ctx:
         keep = ctx.enter_context(tc.tile_pool(name="keep", bufs=1))
-        gelp = ctx.enter_context(tc.tile_pool(name="gelp", bufs=12))
+        gelp = ctx.enter_context(tc.tile_pool(name="gelp", bufs=10))
         hp = ctx.enter_context(tc.tile_pool(name="hp", bufs=3))
-        op = ctx.enter_context(tc.tile_pool(name="op", bufs=1))
-        psum = ctx.enter_context(tc.psum_pool(name="psum", bufs=1))
+        ring = ctx.enter_context(tc.psum_pool(name="ring", bufs=RING))
+        accp = ctx.enter_context(tc.psum_pool(name="accp", bufs=2))
         ctx.enter_context(tc.manual_schedule())
 
         def sb(shape, dt, name):
@@ -40,8 +50,7 @@ def tile_convnext_pointwise_pair_d7_kernel(
 
         ident = sb([P, P], F32, "ident")
         w1s = sb([P, 16], F32, "w1s")
-        w2s_all = sb([P, 4, 16], F32, "w2s_all")
-        w2s = sb([P, 4, 4], F32, "w2s")
+        w2s = sb([P, 64], F32, "w2s")
         g_sb = sb([P, 16], BF16, "g_sb")
         gamma_sb = sb([P, 4, 2], BF16, "gamma_sb")
         y_sb = [sb([P, 2, C], BF16, "y_sb%d" % p) for p in range(4)]
@@ -55,17 +64,17 @@ def tile_convnext_pointwise_pair_d7_kernel(
         w1_scl = [sb([P, 512], U8, "w1_scl%d" % k) for k in range(NG)]
         w2_raw = [sb([P, 2048], U8, "w2_raw%d" % i) for i in range(NI)]
         w2_wide = [sb([P, 2048], BF16, "w2_wide%d" % i) for i in range(NI)]
-        w2_grp = [sb([P, 2048], BF16, "w2_grp%d" % k) for k in range(NG)]
-        w2_codes = [sb([P, 512], U32, "w2_codes%d" % k) for k in range(NG)]
-        w2_scl = [sb([P, 512], U8, "w2_scl%d" % k) for k in range(NG)]
-        h_codes = [[sb([P, 512], U32, "h_codes%d_%d" % (k, n)) for n in range(2)] for k in range(NG)]
-        h_scl = [[sb([P, 512], U8, "h_scl%d_%d" % (k, n)) for n in range(2)] for k in range(NG)]
+        w2_grp = [sb([P, 2048], BF16, "w2_grp%d" % i) for i in range(NI)]
+        w2_codes = [sb([P, 512], U32, "w2_codes%d" % i) for i in range(NI)]
+        w2_scl = [sb([P, 512], U8, "w2_scl%d" % i) for i in range(NI)]
+        h_codes = [sb([P, 512], U32, "h_codes%d" % q) for q in range(8)]
+        h_scl = [sb([P, 512], U8, "h_scl%d" % q) for q in range(8)]
         r_sb = sb([P, NI, NPOS], BF16, "r_sb")
+        o_sb = [sb([P, NI, P * nb], F32, "o_sb%d" % c) for c, (b0, nb) in enumerate(CHUNKS)]
 
         gel = {}
         hbf = {}
         acc = {}
-        tb = {}
 
         def load_w1(k):
             src = w1_bytes.rearrange("(p t) n -> p t n", t=4)[:, :, 512 * k : 512 * (k + 1)]
@@ -79,12 +88,8 @@ def tile_convnext_pointwise_pair_d7_kernel(
         def load_w2(i):
             nc.sync.dma_start(out=w2_raw[i][:], in_=w2_bytes[P * i : P * (i + 1), :])
 
-        def widen(eng, dst, src, lo, hi):
-            d, s = dst[:, lo:hi], src[:, lo:hi].bitcast(FP8)
-            if eng == "s":
-                nc.scalar.copy(out=d, in_=s)
-            else:
-                nc.vector.tensor_copy(out=d, in_=s)
+        def widen(dst, src, lo, hi):
+            nc.scalar.copy(out=dst[:, lo:hi], in_=src[:, lo:hi].bitcast(FP8))
 
         def interleave_w1(k, jb):
             o = w1_grp[k][:].rearrange("p (t m j) -> p m j t", t=4, j=4)[:, 32 * jb : 32 * (jb + 1)]
@@ -93,32 +98,49 @@ def tile_convnext_pointwise_pair_d7_kernel(
                 out=o, in0=i, scalar1=w1s[:, 4 * k + jb : 4 * k + jb + 1], scalar2=None, op0=MULT
             )
 
-        def quant_w1(k):
-            nc.vector.quantize_mx(out=w1_codes[k][:].bitcast(FP8X4), scales=w1_scl[k][:], in_=w1_grp[k][:])
+        def quant(codes, scl, lo, hi, src):
+            nc.vector.quantize_mx(out=codes[:, lo:hi].bitcast(FP8X4), scales=scl[:, lo:hi], in_=src)
 
-        def turn_y(p):
-            t = psum.tile([P, 2, 2, P], F32, name="a%d" % p)
-            words = y_sb[p][:].rearrange("p a k -> p (a k)").bitcast(F32)
+        def quant_w1(k):
+            quant(w1_codes[k], w1_scl[k], 0, 512, w1_grp[k][:])
+
+        def quant_w2(i):
+            quant(w2_codes[i], w2_scl[i], 0, 512, w2_grp[i][:])
+
+        def quant_y(p):
+            quant(y_codes, y_scl, 256 * p, 256 * (p + 1), y_grp[p][:])
+
+        def turn(words):
+            t = ring.tile([P, 2, 2, P], F32, name="bank")
             for a in range(2):
                 for u in range(2):
                     nc.tensor.transpose(t[:, a, u, :], words[:, 256 * a + u : 256 * (a + 1) : 2], ident[:])
             return t
 
-        def exit_y(eng, p, t):
+        def turn_y(p):
+            return turn(y_sb[p][:].rearrange("p a k -> p (a k)").bitcast(F32))
+
+        def exit_y(t, p):
             o = y_grp[p][:].bitcast(F32).rearrange("p (a r u) -> p a r u", a=2, u=2)
-            i = t[:].rearrange("p a u r -> p a r u")
-            if eng == "s":
-                nc.scalar.copy(out=o, in_=i)
-            else:
-                nc.vector.tensor_copy(out=o, in_=i)
+            nc.scalar.copy(out=o, in_=t[:].rearrange("p a u r -> p a r u"))
 
-        def quant_y(p):
-            cols = slice(256 * p, 256 * (p + 1))
-            nc.vector.quantize_mx(out=y_codes[:, cols].bitcast(FP8X4), scales=y_scl[:, cols], in_=y_grp[p][:])
+        def turn_w2(i, half):
+            return turn(w2_wide[i][:, 1024 * half : 1024 * (half + 1)].bitcast(F32))
 
-        def z_unit(u):
-            k, b = divmod(u, 8)
-            z = psum.tile([P, 4, P], F32, name="z%d" % (u % 4))
+        def exit_w2(t, i, half):
+            for a in range(2):
+                k = 2 * half + a
+                o = w2_grp[i][:, 512 * k : 512 * (k + 1)].rearrange("p (r u e) -> p r u e", u=2, e=2)
+                s = t[:, a].rearrange("p u r -> p (u r)").bitcast(BF16).rearrange("p (u r e) -> p r u e", u=2, e=2)
+                col = w2s[:, 16 * i + 4 * k : 16 * i + 4 * k + 1]
+                if 2 * i + half in VEC_EXITS:
+                    nc.vector.tensor_scalar(out=o, in0=s, scalar1=col, scalar2=None, op0=MULT)
+                else:
+                    nc.scalar.activation(out=o, in_=s, func=COPY, scale=col)
+
+        def expand(u):
+            k, b = UNITS[u]
+            z = ring.tile([P, 4, P], F32, name="bank")
             for t in range(4):
                 nc.tensor.matmul_mx(
                     out=z[:, t, :],
@@ -131,161 +153,166 @@ def tile_convnext_pointwise_pair_d7_kernel(
                 )
             return z
 
-        def gelu(u, z):
+        def gelu(z, u):
             a = gelp.tile([P, P, 4], F32, name="gel")
             nc.scalar.activation(out=a[:], in_=z[:].rearrange("p t n -> p n t"), func=GELU)
             gel[u] = a
 
         def gain(u):
-            k = u // 8
+            k = UNITS[u][0]
             if u % 2 == 0:
-                hb = hp.tile([P, 1024], BF16, name="hbf", align_bytes=64)
-                hbf[u // 2] = hb
+                hbf[u // 2] = hp.tile([P, 1024], BF16, name="hbf", align_bytes=64)
             o = hbf[u // 2][:, 512 * (u % 2) : 512 * (u % 2 + 1)].rearrange("p (n t) -> p n t", t=4)
             gk = g_sb[:, 4 * k : 4 * (k + 1)].unsqueeze(1).to_broadcast([P, P, 4])
             nc.vector.tensor_tensor(out=o, in0=gel[u][:], in1=gk, op=MULT)
 
-        def quant_h(pair):
-            k, q = divmod(pair, 4)
-            n, c = divmod(q, 2)
-            cols = slice(256 * c, 256 * (c + 1))
-            nc.vector.quantize_mx(
-                out=h_codes[k][n][:, cols].bitcast(FP8X4), scales=h_scl[k][n][:, cols], in_=hbf[pair][:]
-            )
+        def quant_h(u, n):
+            lo = P * (u % 4)
+            src = hbf[u // 2][:, 512 * (u % 2) : 512 * (u % 2 + n)]
+            quant(h_codes[u // 4], h_scl[u // 4], lo, lo + P * n, src)
 
-        def turn_w2(ip, k, bank):
-            t = psum.tile([P, 2, 2, P], F32, name="a%d" % bank)
-            for ii in range(2):
-                words = w2_wide[2 * ip + ii][:].bitcast(F32)
-                for u in range(2):
-                    nc.tensor.transpose(t[:, ii, u, :], words[:, 256 * k + u : 256 * (k + 1) : 2], ident[:])
-            tb[ip, k] = t
-
-        def exit_w2(eng, i, k):
-            o = w2_grp[k][:, 512 * i : 512 * (i + 1)].rearrange("p (r u e) -> p r u e", u=2, e=2)
-            s = tb[i // 2, k][:, i % 2].rearrange("p u r -> p (u r)").bitcast(BF16)
-            s = s.rearrange("p (u r e) -> p r u e", u=2, e=2)
-            col = w2s[:, i, k : k + 1]
-            if eng == "s":
-                nc.scalar.activation(out=o, in_=s, func=COPY, scale=col)
-            else:
-                nc.vector.tensor_scalar(out=o, in0=s, scalar1=col, scalar2=None, op0=MULT)
-
-        def quant_w2(k):
-            nc.vector.quantize_mx(out=w2_codes[k][:].bitcast(FP8X4), scales=w2_scl[k][:], in_=w2_grp[k][:])
-
-        def stage2(n, i, k):
-            if k == 0:
-                acc[n, i] = psum.tile([P, 512], F32, name=("z%d" if n else "a%d") % i)
+        def contract(c, i, k, start, stop):
+            b0, nb = CHUNKS[c]
+            per_bank = 4 // nb
+            if (c, i // per_bank) not in acc:
+                acc[c, i // per_bank] = (ring if nb == 1 else accp).tile([P, per_bank, P * nb], F32, name="bank")
+            u = UNITS.index((k, b0))
+            cols = slice(P * (u % 4), P * (u % 4 + nb))
             nc.tensor.matmul_mx(
-                out=acc[n, i][:],
-                lhsT=w2_codes[k][:, P * i : P * (i + 1)].bitcast(FP8X4),
-                lhsT_scale=w2_scl[k][:, P * i : P * (i + 1)],
-                rhs=h_codes[k][n][:].bitcast(FP8X4),
-                rhs_scale=h_scl[k][n][:],
-                start=(k == 0),
-                stop=(k == NG - 1),
+                out=acc[c, i // per_bank][:, i % per_bank, :],
+                lhsT=w2_codes[i][:, P * k : P * (k + 1)].bitcast(FP8X4),
+                lhsT_scale=w2_scl[i][:, P * k : P * (k + 1)],
+                rhs=h_codes[u // 4][:, cols].bitcast(FP8X4),
+                rhs_scale=h_scl[u // 4][:, cols],
+                start=start,
+                stop=stop,
             )
 
-        def finish(n, i):
-            o = op.tile([P, 512], F32, name="o%d_%d" % (n, i))
-            cols = slice(512 * n, 512 * (n + 1))
+        def contract_block(c, i):
+            for k in range(NG):
+                contract(c, i, k, k == 0, k == NG - 1)
+
+        def contract_pass(c, k):
+            for i in range(NI):
+                contract(c, i, k, k == 0 and i == 0, k == NG - 1 and i == NI - 1)
+
+        def finish(c, i):
+            b0, nb = CHUNKS[c]
+            per_bank = 4 // nb
+            cols = slice(P * b0, P * (b0 + nb))
             nc.vector.scalar_tensor_tensor(
-                out=o[:], in0=acc[n, i][:], scalar=gamma_sb[:, i, 0:1], in1=r_sb[:, i, cols], op0=MULT, op1=ADD
+                out=o_sb[c][:, i, :],
+                in0=acc[c, i // per_bank][:, i % per_bank, :],
+                scalar=gamma_sb[:, i, 0:1],
+                in1=r_sb[:, i, cols],
+                op0=MULT,
+                op1=ADD,
             )
-            nc.sync.dma_start(out=out[P * i : P * (i + 1), cols], in_=o[:])
+            nc.sync.dma_start(out=out[P * i : P * (i + 1), cols], in_=o_sb[c][:, i, :])
 
         load_w1(0)
+        load_y(0)
         for q in range(4):
             nc.scalar.dma_start(out=w1s[32 * q : 32 * (q + 1), :], in_=w1_scale[q].partition_broadcast(32))
-        for p in range(4):
-            load_y(p)
         load_w1(1)
-        load_w2(0)
-        load_w2(1)
-        load_w1(2)
-        load_w2(2)
-        load_w2(3)
-        load_w1(3)
-        nc.gpsimd.dma_start(out=w2s_all[:], in_=w2_scale.partition_broadcast(P))
+        load_y(1)
         nc.gpsimd.dma_start(out=g_sb[:].rearrange("p (k t) -> p k t", t=4), in_=g.rearrange("(k p t) -> p k t", p=P, t=4))
         make_identity(nc, ident[:])
-        for q in range(4):
-            nc.gpsimd.tensor_copy(
-                out=w2s[32 * q : 32 * (q + 1)],
-                in_=w2s_all[32 * q : 32 * (q + 1)].rearrange("p i (k q) -> p i k q", q=4)[:, :, :, q],
-            )
-        nc.sync.dma_start(out=r_sb[:], in_=r.rearrange("(i p) n -> p i n", p=P))
         nc.gpsimd.dma_start(out=gamma_sb[:, :, 0:1], in_=gamma.rearrange("(i p) -> p i", p=P).unsqueeze(2))
+        load_w1(2)
+        load_w1(3)
+        load_w2(0)
+        w2_flat = w2_scale.rearrange("i j -> (i j)")
+        for q in range(4):
+            nc.sync.dma_start(out=w2s[32 * q : 32 * (q + 1), 0:61], in_=w2_flat[q : q + 61].partition_broadcast(32))
+        load_y(2)
+        load_w2(1)
+        load_y(3)
+        load_w2(2)
+        load_w2(3)
+        nc.sync.dma_start(out=r_sb[:], in_=r.rearrange("(i p) n -> p i n", p=P))
 
-        widen(PLAN["w10"][0], w1_wide[0], w1_raw[0], 0, 1024)
-        widen(PLAN["w10"][1], w1_wide[0], w1_raw[0], 1024, 2048)
+        widen(w1_wide[0], w1_raw[0], 0, 1024)
+        nc.vector.tensor_copy(out=w1_wide[0][:, 1024:2048], in_=w1_raw[0][:, 1024:2048].bitcast(FP8))
+        widen(w1_wide[1], w1_raw[1], 0, 2048)
+        ty = [turn_y(p) for p in range(2)]
+        exit_y(ty[0], 0)
+        exit_y(ty[1], 1)
+        widen(w1_wide[2], w1_raw[2], 0, 2048)
         for jb in range(4):
             interleave_w1(0, jb)
-        ty = [turn_y(p) for p in range(4)]
-        exit_y("s", 0, ty[0])
-        exit_y("s", 1, ty[1])
-        quant_y(0)
         quant_w1(0)
+        interleave_w1(1, 0)
+        quant_y(0)
+        for jb in range(1, 4):
+            interleave_w1(1, jb)
         quant_y(1)
-        z = {}
-        for u in range(3):
-            z[u] = z_unit(u)
+        quant_w1(1)
+        for jb in range(4):
+            interleave_w1(2, jb)
 
-        after = {u: [] for u in range(-1, 33)}
+        banks = {u: [] for u in range(32)}
+        after = {u: [] for u in range(32)}
 
         def put(u, fn, *args):
             after[u].append((fn, args))
 
-        for k in (1, 2, 3):
-            e, s0 = PLAN["w1w"][k]
-            put(s0, widen, e, w1_wide[k], w1_raw[k], 0, 2048)
-        put(-1, exit_y, "s", 2, ty[2])
-        put(-1, exit_y, "s", 3, ty[3])
-        put(-1, quant_y, 2)
-        put(-1, quant_y, 3)
-        for k in (1, 2, 3):
-            for jb in range(4):
-                put(PLAN["w1i"][k][jb], interleave_w1, k, jb)
-            put(PLAN["w1i"][k][3] + 1, quant_w1, k)
-        for i in range(4):
-            e, s0 = PLAN["w2w"][i]
-            put(s0, widen, e, w2_wide[i], w2_raw[i], 0, 2048)
-        order = [(0, k) for k in range(4)] + [(1, k) for k in range(4)]
-        for s, (ip, k) in enumerate(order):
-            u = PLAN["turn"][s]
-            put(u, turn_w2, ip, k, s % 4)
-            e, lag = PLAN["ex"][s]
-            put(u + lag, exit_w2, e, 2 * ip, k)
-            put(u + lag, exit_w2, e, 2 * ip + 1, k)
-            if ip == 1:
-                put(u + lag + 1, quant_w2, k)
-        for k in range(3):
-            for i in range(4):
-                put(PLAN["s2"][k], stage2, 0, i, k)
-        for i in range(4):
-            put(28, stage2, 0, i, 3)
-        for i in range(4):
-            put(PLAN["fin0"][i], finish, 0, i)
-        for k in range(3):
-            for i in range(4):
-                put(PLAN["s2b"] + k, stage2, 1, i, k)
+        put(0, quant_w1, 2)
+        for half in range(2):
+            put(half, widen, w1_wide[3], w1_raw[3], 1024 * half, 1024 * (half + 1))
+        for jb in range(4):
+            put(IL_FIRST + jb, interleave_w1, 3, jb)
+        put(IL_FIRST + 4, quant_w1, 3)
+        for i in range(NI):
+            u = W2_FIRST + W2_PERIOD * i
+            for half in range(2):
+                put(u + half, widen, w2_wide[i], w2_raw[i], 1024 * half, 1024 * (half + 1))
+                banks[u + 4 + half].append((turn_w2, exit_w2, (i, half)))
+            put(u + 7, quant_w2, i)
+        for p in (2, 3):
+            u = 8 * (p - 1) + Y_AT
+            banks[u].append((turn_y, exit_y, (p,)))
+            put(u + 2, quant_y, p)
+        ready = [W2_FIRST + W2_PERIOD * i + 8 for i in range(NI)]
+        for i in range(NI):
+            u = max(18 + 2 * i, ready[i])
+            put(u, contract_block, 0, i)
+            put(u + LAG, finish, 0, i)
+        for pair in range(2):
+            u = max(26, ready[2 * pair + 1] + pair)
+            for i in (2 * pair, 2 * pair + 1):
+                put(u, contract_block, 1, i)
+            for i in (2 * pair, 2 * pair + 1):
+                put(u + LAG, finish, 1, i)
+        for i in range(NI):
+            put(30, contract_block, 2, i)
 
-        for fn, args in after[-1]:
-            fn(*args)
+        jobs = []
         for u in range(32):
-            if u + 3 < 32:
-                z[u + 3] = z_unit(u + 3)
-            gelu(u, z[u])
-            gain(u)
-            if u % 2 == 0 and u:
-                quant_h(u // 2 - 1)
-            for fn, args in after[u]:
-                fn(*args)
-        quant_h(15)
-        for fn, args in after[32]:
-            fn(*args)
-        for i in range(4):
-            stage2(1, i, 3)
-        for i in range(4):
-            finish(1, i)
+            jobs.append((expand, gelu, (u,)))
+            jobs.extend(banks[u])
+        held = {}
+        for j in range(AHEAD):
+            held[j] = jobs[j][0](*jobs[j][2])
+        for j, (fill, empty, args) in enumerate(jobs):
+            if j + AHEAD < len(jobs):
+                held[j + AHEAD] = jobs[j + AHEAD][0](*jobs[j + AHEAD][2])
+            empty(held[j], *args)
+            if fill is expand:
+                u = args[0]
+                gain(u)
+                if u % 2 == 0 and u:
+                    quant_h(u - 2, 2)
+                for fn, fargs in after[u]:
+                    fn(*fargs)
+
+        quant_h(30, 1)
+        for k in range(3):
+            contract_pass(3, k)
+        finish(2, 0)
+        quant_h(31, 1)
+        contract_pass(3, 3)
+        for i in range(1, NI):
+            finish(2, i)
+        for i in range(NI):
+            finish(3, i)

@@ -20,14 +20,8 @@ NG = H // 512
 NI = C // P
 FLOPS = 2 * NPOS * C * H * 2
 
-RING = 6
-AHEAD = 4
-Y_AT = 1
-LAG = 2
-IL_FIRST = 2
-W2_FIRST = 2
-W2_PERIOD = 6
-VEC_EXITS = (1, 3)
+ZRING = 4
+A_FIRST = 17
 
 CHUNKS = ((0, 4), (4, 2), (6, 1), (7, 1))
 UNITS = [(k, b0 + b) for b0, nb in CHUNKS for k in range(NG) for b in range(nb)]
@@ -40,15 +34,18 @@ def tile_convnext_pointwise_pair_d7_kernel(
     with ExitStack() as ctx:
         keep = ctx.enter_context(tc.tile_pool(name="keep", bufs=1))
         gelp = ctx.enter_context(tc.tile_pool(name="gelp", bufs=10))
-        hp = ctx.enter_context(tc.tile_pool(name="hp", bufs=3))
-        ring = ctx.enter_context(tc.psum_pool(name="ring", bufs=RING))
-        accp = ctx.enter_context(tc.psum_pool(name="accp", bufs=2))
+        hp = ctx.enter_context(tc.tile_pool(name="hp", bufs=2))
+        zring = ctx.enter_context(tc.psum_pool(name="zring", bufs=ZRING))
+        tring = ctx.enter_context(tc.psum_pool(name="tring", bufs=3))
+        gpool = ctx.enter_context(tc.psum_pool(name="gpool", bufs=1))
         ctx.enter_context(tc.manual_schedule())
 
         def sb(shape, dt, name):
             return keep.tile(shape, dt, name=name, align_bytes=64)
 
         ident = sb([P, P], F32, "ident")
+        ident16 = sb([P, P], BF16, "ident16")
+        g_ps = gpool.tile([P, 16], F32, name="g_ps")
         w1s = sb([P, 16], F32, "w1s")
         w2s = sb([P, 64], F32, "w2s")
         g_sb = sb([P, 16], BF16, "g_sb")
@@ -59,7 +56,8 @@ def tile_convnext_pointwise_pair_d7_kernel(
         y_scl = sb([P, NPOS], U8, "y_scl")
         w1_raw = [sb([P, 2048], U8, "w1_raw%d" % k) for k in range(NG)]
         w1_wide = [sb([P, 2048], BF16, "w1_wide%d" % k) for k in range(NG)]
-        w1_grp = [sb([P, 2048], BF16, "w1_grp%d" % k) for k in range(NG)]
+        w1_grp = [sb([P, 2048], BF16, "w1_grp%d" % k) for k in range(NG - 1)]
+        w1_grp.append(hp.tile([P, 2048], BF16, name="pool_h", bufs=1, align_bytes=64))
         w1_codes = [sb([P, 512], U32, "w1_codes%d" % k) for k in range(NG)]
         w1_scl = [sb([P, 512], U8, "w1_scl%d" % k) for k in range(NG)]
         w2_raw = [sb([P, 2048], U8, "w2_raw%d" % i) for i in range(NI)]
@@ -75,6 +73,7 @@ def tile_convnext_pointwise_pair_d7_kernel(
         gel = {}
         hbf = {}
         acc = {}
+        turned = {}
 
         def load_w1(k):
             src = w1_bytes.rearrange("(p t) n -> p t n", t=4)[:, :, 512 * k : 512 * (k + 1)]
@@ -110,37 +109,39 @@ def tile_convnext_pointwise_pair_d7_kernel(
         def quant_y(p):
             quant(y_codes, y_scl, 256 * p, 256 * (p + 1), y_grp[p][:])
 
-        def turn(words):
-            t = ring.tile([P, 2, 2, P], F32, name="bank")
+        def turn(key, words):
+            t = tring.tile([P, 2, 2, P], F32, name="bank")
             for a in range(2):
                 for u in range(2):
                     nc.tensor.transpose(t[:, a, u, :], words[:, 256 * a + u : 256 * (a + 1) : 2], ident[:])
-            return t
+            turned[key] = t
 
         def turn_y(p):
-            return turn(y_sb[p][:].rearrange("p a k -> p (a k)").bitcast(F32))
+            turn(("y", p), y_sb[p][:].rearrange("p a k -> p (a k)").bitcast(F32))
 
-        def exit_y(t, p):
+        def exit_y(p):
             o = y_grp[p][:].bitcast(F32).rearrange("p (a r u) -> p a r u", a=2, u=2)
-            nc.scalar.copy(out=o, in_=t[:].rearrange("p a u r -> p a r u"))
+            nc.scalar.copy(out=o, in_=turned["y", p][:].rearrange("p a u r -> p a r u"))
+
+        def widen_w2(i, half):
+            widen(w2_wide[i], w2_raw[i], 1024 * half, 1024 * (half + 1))
 
         def turn_w2(i, half):
-            return turn(w2_wide[i][:, 1024 * half : 1024 * (half + 1)].bitcast(F32))
+            turn((i, half), w2_wide[i][:, 1024 * half : 1024 * (half + 1)].bitcast(F32))
 
-        def exit_w2(t, i, half):
-            for a in range(2):
-                k = 2 * half + a
-                o = w2_grp[i][:, 512 * k : 512 * (k + 1)].rearrange("p (r u e) -> p r u e", u=2, e=2)
-                s = t[:, a].rearrange("p u r -> p (u r)").bitcast(BF16).rearrange("p (u r e) -> p r u e", u=2, e=2)
-                col = w2s[:, 16 * i + 4 * k : 16 * i + 4 * k + 1]
-                if 2 * i + half in VEC_EXITS:
-                    nc.vector.tensor_scalar(out=o, in0=s, scalar1=col, scalar2=None, op0=MULT)
-                else:
-                    nc.scalar.activation(out=o, in_=s, func=COPY, scale=col)
+        def exit_w2(i, k, on_scalar):
+            o = w2_grp[i][:, 512 * k : 512 * (k + 1)].rearrange("p (r u e) -> p r u e", u=2, e=2)
+            s = turned[i, k // 2][:, k % 2].rearrange("p u r -> p (u r)").bitcast(BF16)
+            s = s.rearrange("p (u r e) -> p r u e", u=2, e=2)
+            col = w2s[:, 16 * i + 4 * k : 16 * i + 4 * k + 1]
+            if on_scalar:
+                nc.scalar.activation(out=o, in_=s, func=COPY, scale=col)
+            else:
+                nc.vector.tensor_scalar(out=o, in0=s, scalar1=col, scalar2=None, op0=MULT)
 
         def expand(u):
             k, b = UNITS[u]
-            z = ring.tile([P, 4, P], F32, name="bank")
+            z = zring.tile([P, 4, P], F32, name="bank")
             for t in range(4):
                 nc.tensor.matmul_mx(
                     out=z[:, t, :],
@@ -160,26 +161,32 @@ def tile_convnext_pointwise_pair_d7_kernel(
 
         def gain(u):
             k = UNITS[u][0]
-            if u % 2 == 0:
-                hbf[u // 2] = hp.tile([P, 1024], BF16, name="hbf", align_bytes=64)
-            o = hbf[u // 2][:, 512 * (u % 2) : 512 * (u % 2 + 1)].rearrange("p (n t) -> p n t", t=4)
-            gk = g_sb[:, 4 * k : 4 * (k + 1)].unsqueeze(1).to_broadcast([P, P, 4])
-            nc.vector.tensor_tensor(out=o, in0=gel[u][:], in1=gk, op=MULT)
+            if u % 4 == 0:
+                hbf[u] = hp.tile([P, 512], BF16, name="pool_h", bufs=1, align_bytes=64)[:]
+            elif u % 4 == 1:
+                pair = hp.tile([P, 1024], BF16, name="pair_h", align_bytes=64)
+                hbf[u], hbf[u + 1], hbf[u, u + 1] = pair[:, 0:512], pair[:, 512:1024], pair[:]
+            elif u % 4 == 3:
+                hbf[u] = hp.tile([P, 512], BF16, name="last_h", align_bytes=64)[:]
+            eng, gt = (nc.gpsimd, g_sb) if u % 4 == 0 else (nc.vector, g_ps)
+            gk = gt[:, 4 * k : 4 * (k + 1)].unsqueeze(1).to_broadcast([P, P, 4])
+            eng.tensor_tensor(out=hbf[u].rearrange("p (n t) -> p n t", t=4), in0=gel[u][:], in1=gk, op=MULT)
 
         def quant_h(u, n):
             lo = P * (u % 4)
-            src = hbf[u // 2][:, 512 * (u % 2) : 512 * (u % 2 + n)]
-            quant(h_codes[u // 4], h_scl[u // 4], lo, lo + P * n, src)
+            quant(h_codes[u // 4], h_scl[u // 4], lo, lo + P * n, hbf[u] if n == 1 else hbf[u, u + 1])
+
+        def open_acc(pool, c, blocks):
+            t = pool.tile([P, len(blocks), P * CHUNKS[c][1]], F32, name="bank")
+            for n, i in enumerate(blocks):
+                acc[c, i] = t[:, n, :]
 
         def contract(c, i, k, start, stop):
             b0, nb = CHUNKS[c]
-            per_bank = 4 // nb
-            if (c, i // per_bank) not in acc:
-                acc[c, i // per_bank] = (ring if nb == 1 else accp).tile([P, per_bank, P * nb], F32, name="bank")
             u = UNITS.index((k, b0))
             cols = slice(P * (u % 4), P * (u % 4 + nb))
             nc.tensor.matmul_mx(
-                out=acc[c, i // per_bank][:, i % per_bank, :],
+                out=acc[c, i],
                 lhsT=w2_codes[i][:, P * k : P * (k + 1)].bitcast(FP8X4),
                 lhsT_scale=w2_scl[i][:, P * k : P * (k + 1)],
                 rhs=h_codes[u // 4][:, cols].bitcast(FP8X4),
@@ -188,9 +195,11 @@ def tile_convnext_pointwise_pair_d7_kernel(
                 stop=stop,
             )
 
-        def contract_block(c, i):
-            for k in range(NG):
-                contract(c, i, k, k == 0, k == NG - 1)
+        def contract_blocks(pool, c, blocks):
+            open_acc(pool, c, blocks)
+            for i in blocks:
+                for k in range(NG):
+                    contract(c, i, k, k == 0, k == NG - 1)
 
         def contract_pass(c, k):
             for i in range(NI):
@@ -198,15 +207,9 @@ def tile_convnext_pointwise_pair_d7_kernel(
 
         def finish(c, i):
             b0, nb = CHUNKS[c]
-            per_bank = 4 // nb
             cols = slice(P * b0, P * (b0 + nb))
             nc.vector.scalar_tensor_tensor(
-                out=o_sb[c][:, i, :],
-                in0=acc[c, i // per_bank][:, i % per_bank, :],
-                scalar=gamma_sb[:, i, 0:1],
-                in1=r_sb[:, i, cols],
-                op0=MULT,
-                op1=ADD,
+                out=o_sb[c][:, i, :], in0=acc[c, i], scalar=gamma_sb[:, i, 0:1], in1=r_sb[:, i, cols], op0=MULT, op1=ADD
             )
             nc.sync.dma_start(out=out[P * i : P * (i + 1), cols], in_=o_sb[c][:, i, :])
 
@@ -232,13 +235,17 @@ def tile_convnext_pointwise_pair_d7_kernel(
         load_w2(3)
         nc.sync.dma_start(out=r_sb[:], in_=r.rearrange("(i p) n -> p i n", p=P))
 
+        nc.scalar.copy(out=ident16[:], in_=ident[:])
         widen(w1_wide[0], w1_raw[0], 0, 1024)
         nc.vector.tensor_copy(out=w1_wide[0][:, 1024:2048], in_=w1_raw[0][:, 1024:2048].bitcast(FP8))
         widen(w1_wide[1], w1_raw[1], 0, 2048)
-        ty = [turn_y(p) for p in range(2)]
-        exit_y(ty[0], 0)
-        exit_y(ty[1], 1)
+        turn_y(0)
+        turn_y(1)
+        nc.tensor.matmul(g_ps[:], lhsT=ident16[:], rhs=g_sb[:], start=True, stop=True)
+        exit_y(0)
+        exit_y(1)
         widen(w1_wide[2], w1_raw[2], 0, 2048)
+        widen(w1_wide[3], w1_raw[3], 0, 2048)
         for jb in range(4):
             interleave_w1(0, jb)
         quant_w1(0)
@@ -248,71 +255,86 @@ def tile_convnext_pointwise_pair_d7_kernel(
             interleave_w1(1, jb)
         quant_y(1)
         quant_w1(1)
-        for jb in range(4):
-            interleave_w1(2, jb)
+        for k in (2, 3):
+            for jb in range(4):
+                interleave_w1(k, jb)
+        quant_w1(2)
+        quant_w1(3)
 
-        banks = {u: [] for u in range(32)}
-        after = {u: [] for u in range(32)}
+        side = {u: [] for u in range(32)}
+        batch = {u: [] for u in range(4, 32, 4)}
 
         def put(u, fn, *args):
-            after[u].append((fn, args))
+            side[u].append((fn, args))
 
-        put(0, quant_w1, 2)
-        for half in range(2):
-            put(half, widen, w1_wide[3], w1_raw[3], 1024 * half, 1024 * (half + 1))
-        for jb in range(4):
-            put(IL_FIRST + jb, interleave_w1, 3, jb)
-        put(IL_FIRST + 4, quant_w1, 3)
-        for i in range(NI):
-            u = W2_FIRST + W2_PERIOD * i
+        for i in range(2):
             for half in range(2):
-                put(u + half, widen, w2_wide[i], w2_raw[i], 1024 * half, 1024 * (half + 1))
-                banks[u + 4 + half].append((turn_w2, exit_w2, (i, half)))
-            put(u + 7, quant_w2, i)
-        for p in (2, 3):
-            u = 8 * (p - 1) + Y_AT
-            banks[u].append((turn_y, exit_y, (p,)))
-            put(u + 2, quant_y, p)
-        ready = [W2_FIRST + W2_PERIOD * i + 8 for i in range(NI)]
-        for i in range(NI):
-            u = max(18 + 2 * i, ready[i])
-            put(u, contract_block, 0, i)
-            put(u + LAG, finish, 0, i)
-        for pair in range(2):
-            u = max(26, ready[2 * pair + 1] + pair)
-            for i in (2 * pair, 2 * pair + 1):
-                put(u, contract_block, 1, i)
-            for i in (2 * pair, 2 * pair + 1):
-                put(u + LAG, finish, 1, i)
-        for i in range(NI):
-            put(30, contract_block, 2, i)
+                put(4 * i + half, widen_w2, i, half)
+                put(4 * i + half + 1, turn_w2, i, half)
+                put(4 * i + half + 2, exit_w2, i, 2 * half, False)
+                put(4 * i + half + 2, exit_w2, i, 2 * half + 1, False)
+            batch[4 * i + 4].append((quant_w2, (i,)))
+        put(3, turn_y, 2)
+        put(6, exit_y, 2)
+        batch[12].append((quant_y, (2,)))
+        put(9, widen_w2, 2, 0)
+        put(10, turn_w2, 2, 0)
+        put(10, widen_w2, 2, 1)
+        put(11, turn_w2, 2, 1)
+        put(12, exit_w2, 2, 0, False)
+        put(13, exit_w2, 2, 1, False)
+        put(13, exit_w2, 2, 2, True)
+        put(14, exit_w2, 2, 3, True)
+        batch[16].append((quant_w2, (2,)))
+        put(14, turn_y, 3)
+        put(16, exit_y, 3)
+        batch[20].append((quant_y, (3,)))
+        put(17, widen_w2, 3, 0)
+        put(18, turn_w2, 3, 0)
+        put(19, widen_w2, 3, 1)
+        put(21, turn_w2, 3, 1)
+        for k in range(4):
+            put(20 + k + k // 2, exit_w2, 3, k, True)
+        batch[28].append((quant_w2, (3,)))
+        for i in range(3):
+            put(A_FIRST + 2 * i, contract_blocks, tring, 0, [i])
+            put(A_FIRST + 2 * i + 2, finish, 0, i)
+        put(25, contract_blocks, tring, 1, [0, 1])
+        put(26, contract_blocks, tring, 1, [2])
+        put(26, finish, 1, 0)
+        put(27, finish, 1, 1)
+        put(27, finish, 1, 2)
+        put(28, contract_blocks, tring, 0, [3])
+        put(29, contract_blocks, tring, 2, range(NI))
+        put(29, contract_blocks, tring, 1, [3])
+        put(30, finish, 0, 3)
+        put(30, open_acc, zring, 3, range(NI))
+        put(30, finish, 2, 0)
+        put(30, quant_h, 29, 2)
+        put(30, quant_h, 28, 1)
+        for k in range(NG - 1):
+            put(30, contract_pass, 3, k)
+        put(31, finish, 2, 1)
 
-        jobs = []
+        z = {u: expand(u) for u in range(ZRING - 1)}
         for u in range(32):
-            jobs.append((expand, gelu, (u,)))
-            jobs.extend(banks[u])
-        held = {}
-        for j in range(AHEAD):
-            held[j] = jobs[j][0](*jobs[j][2])
-        for j, (fill, empty, args) in enumerate(jobs):
-            if j + AHEAD < len(jobs):
-                held[j + AHEAD] = jobs[j + AHEAD][0](*jobs[j + AHEAD][2])
-            empty(held[j], *args)
-            if fill is expand:
-                u = args[0]
-                gain(u)
-                if u % 2 == 0 and u:
-                    quant_h(u - 2, 2)
-                for fn, fargs in after[u]:
-                    fn(*fargs)
+            if u + ZRING - 1 < 32:
+                z[u + ZRING - 1] = expand(u + ZRING - 1)
+            gelu(z[u], u)
+            if u in batch:
+                quant_h(u - 3, 2)
+                for fn, args in batch[u]:
+                    fn(*args)
+                quant_h(u - 1, 1)
+                quant_h(u - 4, 1)
+            gain(u)
+            for fn, args in side[u]:
+                fn(*args)
 
-        quant_h(30, 1)
-        for k in range(3):
-            contract_pass(3, k)
-        finish(2, 0)
         quant_h(31, 1)
-        contract_pass(3, 3)
-        for i in range(1, NI):
+        contract_pass(3, NG - 1)
+        finish(1, 3)
+        for i in range(2, NI):
             finish(2, i)
         for i in range(NI):
             finish(3, i)

@@ -21,7 +21,13 @@ NI = C // P
 FLOPS = 2 * NPOS * C * H * 2
 
 ZRING = 4
-A_FIRST = 17
+VRING = 3
+POOL_COLS = 768
+WIDEN_AHEAD = 2
+FIN = 2
+B_AT = 26
+STORE = (1, 1, 2, 2)
+W3_AT = 11
 
 CHUNKS = ((0, 4), (4, 2), (6, 1), (7, 1))
 UNITS = [(k, b0 + b) for b0, nb in CHUNKS for k in range(NG) for b in range(nb)]
@@ -33,10 +39,10 @@ def tile_convnext_pointwise_pair_d7_kernel(
     nc = tc.nc
     with ExitStack() as ctx:
         keep = ctx.enter_context(tc.tile_pool(name="keep", bufs=1))
-        gelp = ctx.enter_context(tc.tile_pool(name="gelp", bufs=10))
+        gelp = ctx.enter_context(tc.tile_pool(name="gelp", bufs=3))
         hp = ctx.enter_context(tc.tile_pool(name="hp", bufs=2))
         zring = ctx.enter_context(tc.psum_pool(name="zring", bufs=ZRING))
-        tring = ctx.enter_context(tc.psum_pool(name="tring", bufs=3))
+        vring = ctx.enter_context(tc.psum_pool(name="vring", bufs=VRING))
         gpool = ctx.enter_context(tc.psum_pool(name="gpool", bufs=1))
         ctx.enter_context(tc.manual_schedule())
 
@@ -109,32 +115,37 @@ def tile_convnext_pointwise_pair_d7_kernel(
         def quant_y(p):
             quant(y_codes, y_scl, 256 * p, 256 * (p + 1), y_grp[p][:])
 
-        def turn(key, words):
-            t = tring.tile([P, 2, 2, P], F32, name="bank")
+        def lay_w1(k, half):
+            interleave_w1(k, 2 * half)
+            interleave_w1(k, 2 * half + 1)
+
+        def turn(pool, words):
+            t = pool.tile([P, 2, 2, P], F32, name="bank")
             for a in range(2):
                 for u in range(2):
                     nc.tensor.transpose(t[:, a, u, :], words[:, 256 * a + u : 256 * (a + 1) : 2], ident[:])
-            turned[key] = t
+            return t
 
         def turn_y(p):
-            turn(("y", p), y_sb[p][:].rearrange("p a k -> p (a k)").bitcast(F32))
+            return turn(zring, y_sb[p][:].rearrange("p a k -> p (a k)").bitcast(F32))
 
-        def exit_y(p):
+        def exit_y(t, p):
             o = y_grp[p][:].bitcast(F32).rearrange("p (a r u) -> p a r u", a=2, u=2)
-            nc.scalar.copy(out=o, in_=turned["y", p][:].rearrange("p a u r -> p a r u"))
+            nc.scalar.copy(out=o, in_=t[:].rearrange("p a u r -> p a r u"))
 
         def widen_w2(i, half):
             widen(w2_wide[i], w2_raw[i], 1024 * half, 1024 * (half + 1))
 
         def turn_w2(i, half):
-            turn((i, half), w2_wide[i][:, 1024 * half : 1024 * (half + 1)].bitcast(F32))
+            pool = zring if i == NI - 1 else vring
+            turned["w2", i, half] = turn(pool, w2_wide[i][:, 1024 * half : 1024 * (half + 1)].bitcast(F32))
 
-        def exit_w2(i, k, on_scalar):
+        def exit_w2(i, k):
             o = w2_grp[i][:, 512 * k : 512 * (k + 1)].rearrange("p (r u e) -> p r u e", u=2, e=2)
-            s = turned[i, k // 2][:, k % 2].rearrange("p u r -> p (u r)").bitcast(BF16)
+            s = turned["w2", i, k // 2][:, k % 2].rearrange("p u r -> p (u r)").bitcast(BF16)
             s = s.rearrange("p (u r e) -> p r u e", u=2, e=2)
             col = w2s[:, 16 * i + 4 * k : 16 * i + 4 * k + 1]
-            if on_scalar:
+            if i == NI - 1:
                 nc.scalar.activation(out=o, in_=s, func=COPY, scale=col)
             else:
                 nc.vector.tensor_scalar(out=o, in0=s, scalar1=col, scalar2=None, op0=MULT)
@@ -155,26 +166,35 @@ def tile_convnext_pointwise_pair_d7_kernel(
             return z
 
         def gelu(z, u):
-            a = gelp.tile([P, P, 4], F32, name="gel")
-            nc.scalar.activation(out=a[:], in_=z[:].rearrange("p t n -> p n t"), func=GELU)
-            gel[u] = a
+            if u % 4 == 0:
+                gel[u // 4] = gelp.tile([P, 2048], F32, name="gel")
+            a = gel[u // 4][:, 512 * (u % 4) : 512 * (u % 4 + 1)].rearrange("p (n t) -> p n t", t=4)
+            nc.scalar.activation(out=a, in_=z[:].rearrange("p t n -> p n t"), func=GELU)
+
+        def pool_cols(q):
+            return POOL_COLS if UNITS[4 * q][0] == UNITS[4 * q + 1][0] else 512
+
+        def gain_cols(eng, gt, dst, q, lo, hi):
+            k = UNITS[4 * q + lo // 512][0]
+            gk = gt[:, 4 * k : 4 * (k + 1)].unsqueeze(1).to_broadcast([P, (hi - lo) // 4, 4])
+            a = gel[q][:, lo:hi].rearrange("p (n t) -> p n t", t=4)
+            eng.tensor_tensor(out=dst.rearrange("p (n t) -> p n t", t=4), in0=a, in1=gk, op=MULT)
 
         def gain(u):
-            k = UNITS[u][0]
-            if u % 4 == 0:
-                hbf[u] = hp.tile([P, 512], BF16, name="pool_h", bufs=1, align_bytes=64)[:]
-            elif u % 4 == 1:
-                pair = hp.tile([P, 1024], BF16, name="pair_h", align_bytes=64)
-                hbf[u], hbf[u + 1], hbf[u, u + 1] = pair[:, 0:512], pair[:, 512:1024], pair[:]
-            elif u % 4 == 3:
-                hbf[u] = hp.tile([P, 512], BF16, name="last_h", align_bytes=64)[:]
-            eng, gt = (nc.gpsimd, g_sb) if u % 4 == 0 else (nc.vector, g_ps)
-            gk = gt[:, 4 * k : 4 * (k + 1)].unsqueeze(1).to_broadcast([P, P, 4])
-            eng.tensor_tensor(out=hbf[u].rearrange("p (n t) -> p n t", t=4), in0=gel[u][:], in1=gk, op=MULT)
+            q, pc = u // 4, pool_cols(u // 4)
+            if u % 4 == (pc - 1) // 512:
+                hbf["pool", q] = hp.tile([P, pc], BF16, name="pool_h", bufs=1, align_bytes=64)
+                gain_cols(nc.gpsimd, g_sb, hbf["pool", q][:], q, 0, pc)
+            if u % 4 == 1:
+                hbf[q] = hp.tile([P, 2048], BF16, name="vec_h", align_bytes=64)
+            lo, hi = max(pc, 512 * (u % 4)), 512 * (u % 4 + 1)
+            if lo < hi:
+                gain_cols(nc.vector, g_ps, hbf[q][:, lo:hi], q, lo, hi)
 
-        def quant_h(u, n):
-            lo = P * (u % 4)
-            quant(h_codes[u // 4], h_scl[u // 4], lo, lo + P * n, hbf[u] if n == 1 else hbf[u, u + 1])
+        def quant_h(q, lo, hi):
+            src = hbf["pool", q] if lo < pool_cols(q) else hbf[q]
+            if lo < hi:
+                quant(h_codes[q], h_scl[q], lo // 4, hi // 4, src[:, lo:hi])
 
         def open_acc(pool, c, blocks):
             t = pool.tile([P, len(blocks), P * CHUNKS[c][1]], F32, name="bank")
@@ -201,9 +221,9 @@ def tile_convnext_pointwise_pair_d7_kernel(
                 for k in range(NG):
                     contract(c, i, k, k == 0, k == NG - 1)
 
-        def contract_pass(c, k):
+        def contract_pass(c, k, first, last):
             for i in range(NI):
-                contract(c, i, k, k == 0 and i == 0, k == NG - 1 and i == NI - 1)
+                contract(c, i, k, first and i % 2 == 0, last and i % 2 == 1)
 
         def finish(c, i):
             b0, nb = CHUNKS[c]
@@ -211,19 +231,21 @@ def tile_convnext_pointwise_pair_d7_kernel(
             nc.vector.scalar_tensor_tensor(
                 out=o_sb[c][:, i, :], in0=acc[c, i], scalar=gamma_sb[:, i, 0:1], in1=r_sb[:, i, cols], op0=MULT, op1=ADD
             )
-            nc.sync.dma_start(out=out[P * i : P * (i + 1), cols], in_=o_sb[c][:, i, :])
+            n = STORE[c]
+            if i % n == n - 1:
+                rows = out[P * (i + 1 - n) : P * (i + 1), cols].rearrange("(i p) n -> p i n", p=P)
+                nc.sync.dma_start(out=rows, in_=o_sb[c][:, i + 1 - n : i + 1, :])
 
         load_w1(0)
-        load_y(0)
+        load_w1(1)
         for q in range(4):
             nc.scalar.dma_start(out=w1s[32 * q : 32 * (q + 1), :], in_=w1_scale[q].partition_broadcast(32))
-        load_w1(1)
-        load_y(1)
-        nc.gpsimd.dma_start(out=g_sb[:].rearrange("p (k t) -> p k t", t=4), in_=g.rearrange("(k p t) -> p k t", p=P, t=4))
-        make_identity(nc, ident[:])
-        nc.gpsimd.dma_start(out=gamma_sb[:, :, 0:1], in_=gamma.rearrange("(i p) -> p i", p=P).unsqueeze(2))
         load_w1(2)
+        load_y(0)
+        make_identity(nc, ident[:])
         load_w1(3)
+        load_y(1)
+        nc.sync.dma_start(out=g_sb[:].rearrange("p (k t) -> p k t", t=4), in_=g.rearrange("(k p t) -> p k t", p=P, t=4))
         load_w2(0)
         w2_flat = w2_scale.rearrange("i j -> (i j)")
         for q in range(4):
@@ -234,107 +256,108 @@ def tile_convnext_pointwise_pair_d7_kernel(
         load_w2(2)
         load_w2(3)
         nc.sync.dma_start(out=r_sb[:], in_=r.rearrange("(i p) n -> p i n", p=P))
+        nc.sync.dma_start(out=gamma_sb[:, :, 0:1], in_=gamma.rearrange("(i p) -> p i", p=P).unsqueeze(2))
 
         nc.scalar.copy(out=ident16[:], in_=ident[:])
         widen(w1_wide[0], w1_raw[0], 0, 1024)
         nc.vector.tensor_copy(out=w1_wide[0][:, 1024:2048], in_=w1_raw[0][:, 1024:2048].bitcast(FP8))
-        widen(w1_wide[1], w1_raw[1], 0, 2048)
-        turn_y(0)
-        turn_y(1)
-        nc.tensor.matmul(g_ps[:], lhsT=ident16[:], rhs=g_sb[:], start=True, stop=True)
-        exit_y(0)
-        exit_y(1)
-        widen(w1_wide[2], w1_raw[2], 0, 2048)
-        widen(w1_wide[3], w1_raw[3], 0, 2048)
-        for jb in range(4):
-            interleave_w1(0, jb)
+        for k in range(1, NG):
+            widen(w1_wide[k], w1_raw[k], 0, 2048)
+        ty = [turn_y(0), turn_y(1)]
+        exit_y(ty[0], 0)
+        exit_y(ty[1], 1)
+        widen_w2(0, 0)
+        lay_w1(0, 0)
+        lay_w1(0, 1)
+        lay_w1(1, 0)
         quant_w1(0)
-        interleave_w1(1, 0)
+        lay_w1(1, 1)
+        lay_w1(2, 0)
         quant_y(0)
-        for jb in range(1, 4):
-            interleave_w1(1, jb)
-        quant_y(1)
         quant_w1(1)
-        for k in (2, 3):
-            for jb in range(4):
-                interleave_w1(k, jb)
-        quant_w1(2)
-        quant_w1(3)
+        quant_y(1)
 
         side = {u: [] for u in range(32)}
+        zside = {u: [] for u in range(32)}
         batch = {u: [] for u in range(4, 32, 4)}
 
         def put(u, fn, *args):
             side[u].append((fn, args))
 
-        for i in range(2):
-            for half in range(2):
-                put(4 * i + half, widen_w2, i, half)
-                put(4 * i + half + 1, turn_w2, i, half)
-                put(4 * i + half + 2, exit_w2, i, 2 * half, False)
-                put(4 * i + half + 2, exit_w2, i, 2 * half + 1, False)
-            batch[4 * i + 4].append((quant_w2, (i,)))
-        put(3, turn_y, 2)
-        put(6, exit_y, 2)
-        batch[12].append((quant_y, (2,)))
-        put(9, widen_w2, 2, 0)
-        put(10, turn_w2, 2, 0)
-        put(10, widen_w2, 2, 1)
-        put(11, turn_w2, 2, 1)
-        put(12, exit_w2, 2, 0, False)
-        put(13, exit_w2, 2, 1, False)
-        put(13, exit_w2, 2, 2, True)
-        put(14, exit_w2, 2, 3, True)
-        batch[16].append((quant_w2, (2,)))
-        put(14, turn_y, 3)
-        put(16, exit_y, 3)
-        batch[20].append((quant_y, (3,)))
-        put(17, widen_w2, 3, 0)
-        put(18, turn_w2, 3, 0)
-        put(19, widen_w2, 3, 1)
-        put(21, turn_w2, 3, 1)
-        for k in range(4):
-            put(20 + k + k // 2, exit_w2, 3, k, True)
-        batch[28].append((quant_w2, (3,)))
-        for i in range(3):
-            put(A_FIRST + 2 * i, contract_blocks, tring, 0, [i])
-            put(A_FIRST + 2 * i + 2, finish, 0, i)
-        put(25, contract_blocks, tring, 1, [0, 1])
-        put(26, contract_blocks, tring, 1, [2])
-        put(26, finish, 1, 0)
-        put(27, finish, 1, 1)
-        put(27, finish, 1, 2)
-        put(28, contract_blocks, tring, 0, [3])
-        put(29, contract_blocks, tring, 2, range(NI))
-        put(29, contract_blocks, tring, 1, [3])
-        put(30, finish, 0, 3)
-        put(30, open_acc, zring, 3, range(NI))
-        put(30, finish, 2, 0)
-        put(30, quant_h, 29, 2)
-        put(30, quant_h, 28, 1)
-        for k in range(NG - 1):
-            put(30, contract_pass, 3, k)
-        put(31, finish, 2, 1)
+        def empty_w2(t, i, half):
+            exit_w2(i, 2 * half)
+            exit_w2(i, 2 * half + 1)
 
-        z = {u: expand(u) for u in range(ZRING - 1)}
+        for n in range(NG * (NI - 1)):
+            i, k = divmod(n, NG)
+            u = n + n // 3 + 1
+            if k % 2 == 0:
+                if n:
+                    put(u - WIDEN_AHEAD, widen_w2, i, k // 2)
+                put(u - 1, turn_w2, i, k // 2)
+            put(u, exit_w2, i, k)
+            if k == NG - 1:
+                batch[4 * (u // 4) + 4].append((quant_w2, (i,)))
+        for p in (2, 3):
+            zside[8 * p - 11].append((turn_y, exit_y, (p,)))
+            batch[8 * p - 8].append((quant_y, (p,)))
+        for half in range(2):
+            put(W3_AT + 2 * half, widen_w2, NI - 1, half)
+            zside[W3_AT + 5 + 2 * half].append((turn_w2, empty_w2, (NI - 1, half)))
+        batch[20].append((quant_w2, (NI - 1,)))
+        for i in range(NI):
+            u = 17 + 4 * (i // 2) + i % 2
+            put(u, contract_blocks, vring, 0, [i])
+            put(u + FIN, finish, 0, i)
+        for pair in range(2):
+            put(B_AT + pair, contract_blocks, vring, 1, [2 * pair, 2 * pair + 1])
+        put(B_AT + 1, finish, 1, 0)
+        put(B_AT + 2, finish, 1, 1)
+        put(29, contract_blocks, vring, 2, range(NI))
+        put(30, finish, 1, 2)
+        put(30, quant_h, 7, 512, 1536)
+        for pair in range(2):
+            put(30, open_acc, zring, 3, [2 * pair, 2 * pair + 1])
+        put(30, contract_pass, 3, 1, True, False)
+        put(30, contract_pass, 3, 2, False, False)
+
+        jobs = []
         for u in range(32):
-            if u + ZRING - 1 < 32:
-                z[u + ZRING - 1] = expand(u + ZRING - 1)
-            gelu(z[u], u)
+            jobs.append((expand, gelu, (u,)))
+            jobs.extend(zside[u])
+        held = {j: jobs[j][0](*jobs[j][2]) for j in range(ZRING - 1)}
+        nc.tensor.matmul(g_ps[:], lhsT=ident16[:], rhs=g_sb[:], start=True, stop=True)
+        lay_w1(2, 1)
+        lay_w1(3, 0)
+        lay_w1(3, 1)
+        quant_w1(2)
+        quant_w1(3)
+        for j, (fill, empty, args) in enumerate(jobs):
+            if j + ZRING - 1 < len(jobs):
+                held[j + ZRING - 1] = jobs[j + ZRING - 1][0](*jobs[j + ZRING - 1][2])
+            empty(held[j], *args)
+            if fill is not expand:
+                continue
+            u = args[0]
             if u in batch:
-                quant_h(u - 3, 2)
-                for fn, args in batch[u]:
-                    fn(*args)
-                quant_h(u - 1, 1)
-                quant_h(u - 4, 1)
+                q = u // 4 - 1
+                quant_h(q, pool_cols(q), 1024)
+                quant_h(q, 1024, 1536)
+                for fn, fargs in batch[u]:
+                    fn(*fargs)
+                quant_h(q, 1536, 2048)
+                quant_h(q, 0, 512)
+                quant_h(q, 512, pool_cols(q))
             gain(u)
-            for fn, args in side[u]:
-                fn(*args)
+            for fn, fargs in side[u]:
+                fn(*fargs)
 
-        quant_h(31, 1)
-        contract_pass(3, NG - 1)
+        quant_h(7, 0, 512)
+        contract_pass(3, 0, False, False)
         finish(1, 3)
-        for i in range(2, NI):
+        quant_h(7, 1536, 2048)
+        contract_pass(3, NG - 1, False, True)
+        for i in range(NI):
             finish(2, i)
         for i in range(NI):
             finish(3, i)

@@ -22,11 +22,26 @@ FLOPS = 2 * NPOS * C * H * 2
 
 ZRING = 4
 VRING = 3
-POOL_COLS = 768
+POOL_POS = 96
+LAST_POS = 72
+X_AT = 1
+S_EARLY = 0
+XN = 14
+VEC_EXITS = 14
+S_LAY = 1
+B2_AT = 29
+B3_AT = 29
+C_EARLY = 0
+C_AT = 29
 WIDEN_AHEAD = 2
 FIN = 2
+A_AT = 17
+LAG = 0
+Y_AT = 10
+X3 = 5
+Q3 = 20
 B_AT = 26
-STORE = (1, 1, 2, 2)
+STORE = (1, 1, 1, 1)
 W3_AT = 11
 
 CHUNKS = ((0, 4), (4, 2), (6, 1), (7, 1))
@@ -62,8 +77,8 @@ def tile_convnext_pointwise_pair_d7_kernel(
         y_scl = sb([P, NPOS], U8, "y_scl")
         w1_raw = [sb([P, 2048], U8, "w1_raw%d" % k) for k in range(NG)]
         w1_wide = [sb([P, 2048], BF16, "w1_wide%d" % k) for k in range(NG)]
-        w1_grp = [sb([P, 2048], BF16, "w1_grp%d" % k) for k in range(NG - 1)]
-        w1_grp.append(hp.tile([P, 2048], BF16, name="pool_h", bufs=1, align_bytes=64))
+        w1_grp = {k: sb([P, 2048], BF16, "w1_grp%d" % k) for k in (0, 1, 3)}
+        w1_grp[2] = hp.tile([P, 2048], BF16, name="pool_h", bufs=1, align_bytes=64)
         w1_codes = [sb([P, 512], U32, "w1_codes%d" % k) for k in range(NG)]
         w1_scl = [sb([P, 512], U8, "w1_scl%d" % k) for k in range(NG)]
         w2_raw = [sb([P, 2048], U8, "w2_raw%d" % i) for i in range(NI)]
@@ -99,9 +114,11 @@ def tile_convnext_pointwise_pair_d7_kernel(
         def interleave_w1(k, jb):
             o = w1_grp[k][:].rearrange("p (t m j) -> p m j t", t=4, j=4)[:, 32 * jb : 32 * (jb + 1)]
             i = w1_wide[k][:].rearrange("p (j m t) -> p m j t", j=4, t=4)[:, 32 * jb : 32 * (jb + 1)]
-            nc.vector.tensor_scalar(
-                out=o, in0=i, scalar1=w1s[:, 4 * k + jb : 4 * k + jb + 1], scalar2=None, op0=MULT
-            )
+            col = w1s[:, 4 * k + jb : 4 * k + jb + 1]
+            if 4 * k + jb >= 16 - S_LAY or (k == 1 and jb == 3 and S_EARLY):
+                nc.scalar.activation(out=o, in_=i, func=COPY, scale=col)
+            else:
+                nc.vector.tensor_scalar(out=o, in0=i, scalar1=col, scalar2=None, op0=MULT)
 
         def quant(codes, scl, lo, hi, src):
             nc.vector.quantize_mx(out=codes[:, lo:hi].bitcast(FP8X4), scales=scl[:, lo:hi], in_=src)
@@ -137,7 +154,7 @@ def tile_convnext_pointwise_pair_d7_kernel(
             widen(w2_wide[i], w2_raw[i], 1024 * half, 1024 * (half + 1))
 
         def turn_w2(i, half):
-            pool = zring if i == NI - 1 else vring
+            pool = zring if NG * i + 2 * half >= VEC_EXITS else vring
             turned["w2", i, half] = turn(pool, w2_wide[i][:, 1024 * half : 1024 * (half + 1)].bitcast(F32))
 
         def exit_w2(i, k):
@@ -145,7 +162,7 @@ def tile_convnext_pointwise_pair_d7_kernel(
             s = turned["w2", i, k // 2][:, k % 2].rearrange("p u r -> p (u r)").bitcast(BF16)
             s = s.rearrange("p (u r e) -> p r u e", u=2, e=2)
             col = w2s[:, 16 * i + 4 * k : 16 * i + 4 * k + 1]
-            if i == NI - 1:
+            if NG * i + k >= VEC_EXITS:
                 nc.scalar.activation(out=o, in_=s, func=COPY, scale=col)
             else:
                 nc.vector.tensor_scalar(out=o, in0=s, scalar1=col, scalar2=None, op0=MULT)
@@ -168,33 +185,33 @@ def tile_convnext_pointwise_pair_d7_kernel(
         def gelu(z, u):
             if u % 4 == 0:
                 gel[u // 4] = gelp.tile([P, 2048], F32, name="gel")
-            a = gel[u // 4][:, 512 * (u % 4) : 512 * (u % 4 + 1)].rearrange("p (n t) -> p n t", t=4)
-            nc.scalar.activation(out=a, in_=z[:].rearrange("p t n -> p n t"), func=GELU)
+            a = gel[u // 4][:, 512 * (u % 4) : 512 * (u % 4 + 1)]
+            nc.scalar.activation(out=a.rearrange("p (n t) -> p n t", t=4), in_=z[:].rearrange("p t n -> p n t"), func=GELU)
 
-        def pool_cols(q):
-            return POOL_COLS if UNITS[4 * q][0] == UNITS[4 * q + 1][0] else 512
+        def gain_of(gt, u, n, npos):
+            k0, k1 = UNITS[u][0], UNITS[u + n - 1][0]
+            gk = gt[:, 4 * k0 : 4 * (k1 + 1)].rearrange("p (k t) -> p k t", t=4)
+            return gk.unsqueeze(2).to_broadcast([P, n, npos, 4])
 
-        def gain_cols(eng, gt, dst, q, lo, hi):
-            k = UNITS[4 * q + lo // 512][0]
-            gk = gt[:, 4 * k : 4 * (k + 1)].unsqueeze(1).to_broadcast([P, (hi - lo) // 4, 4])
-            a = gel[q][:, lo:hi].rearrange("p (n t) -> p n t", t=4)
-            eng.tensor_tensor(out=dst.rearrange("p (n t) -> p n t", t=4), in0=a, in1=gk, op=MULT)
+        def gain_part(eng, gt, dst, u, n, lo, hi):
+            a = gel[u // 4][:].rearrange("p (u n t) -> p u n t", u=4, t=4)[:, u % 4 : u % 4 + n, lo:hi]
+            eng.tensor_tensor(out=dst[:, :, lo:hi], in0=a, in1=gain_of(gt, u, n, hi - lo), op=MULT)
 
         def gain(u):
-            q, pc = u // 4, pool_cols(u // 4)
-            if u % 4 == (pc - 1) // 512:
-                hbf["pool", q] = hp.tile([P, pc], BF16, name="pool_h", bufs=1, align_bytes=64)
-                gain_cols(nc.gpsimd, g_sb, hbf["pool", q][:], q, 0, pc)
             if u % 4 == 1:
-                hbf[q] = hp.tile([P, 2048], BF16, name="vec_h", align_bytes=64)
-            lo, hi = max(pc, 512 * (u % 4)), 512 * (u % 4 + 1)
-            if lo < hi:
-                gain_cols(nc.vector, g_ps, hbf[q][:, lo:hi], q, lo, hi)
+                hbf[u - 1] = hp.tile([P, 2, P, 4], BF16, name="pool_h", bufs=1, align_bytes=64)
+                cut = LAST_POS if u > 28 else POOL_POS
+                gain_part(nc.gpsimd, g_sb, hbf[u - 1], u - 1, 2, 0, cut)
+                gain_part(nc.vector, g_ps, hbf[u - 1], u - 1, 2, cut, P)
+            elif u % 4 > 1:
+                if u % 4 == 2:
+                    hbf[u] = hp.tile([P, 2, P, 4], BF16, name="vec_h", align_bytes=64)
+                dst = hbf[u - u % 2][:, u % 2 : u % 2 + 1]
+                gain_part(nc.vector, g_ps, dst, u, 1, 0, P)
 
-        def quant_h(q, lo, hi):
-            src = hbf["pool", q] if lo < pool_cols(q) else hbf[q]
-            if lo < hi:
-                quant(h_codes[q], h_scl[q], lo // 4, hi // 4, src[:, lo:hi])
+        def quant_h(u, n):
+            src = hbf[u - u % 2][:, u % 2 : u % 2 + n].rearrange("p u n t -> p (u n t)")
+            quant(h_codes[u // 4], h_scl[u // 4], P * (u % 4), P * (u % 4 + n), src)
 
         def open_acc(pool, c, blocks):
             t = pool.tile([P, len(blocks), P * CHUNKS[c][1]], F32, name="bank")
@@ -263,15 +280,21 @@ def tile_convnext_pointwise_pair_d7_kernel(
         nc.vector.tensor_copy(out=w1_wide[0][:, 1024:2048], in_=w1_raw[0][:, 1024:2048].bitcast(FP8))
         for k in range(1, NG):
             widen(w1_wide[k], w1_raw[k], 0, 2048)
+            if k == 1 and S_EARLY:
+                interleave_w1(1, 3)
         ty = [turn_y(0), turn_y(1)]
         exit_y(ty[0], 0)
         exit_y(ty[1], 1)
+        for jb in range(4 - S_LAY, 4):
+            interleave_w1(3, jb)
         widen_w2(0, 0)
         lay_w1(0, 0)
         lay_w1(0, 1)
         lay_w1(1, 0)
         quant_w1(0)
-        lay_w1(1, 1)
+        interleave_w1(1, 2)
+        if not S_EARLY:
+            interleave_w1(1, 3)
         lay_w1(2, 0)
         quant_y(0)
         quant_w1(1)
@@ -279,6 +302,7 @@ def tile_convnext_pointwise_pair_d7_kernel(
 
         side = {u: [] for u in range(32)}
         zside = {u: [] for u in range(32)}
+        sside = {u: [] for u in range(32)}
         batch = {u: [] for u in range(4, 32, 4)}
 
         def put(u, fn, *args):
@@ -288,38 +312,55 @@ def tile_convnext_pointwise_pair_d7_kernel(
             exit_w2(i, 2 * half)
             exit_w2(i, 2 * half + 1)
 
-        for n in range(NG * (NI - 1)):
+        ready = [Q3 + 1] * NI
+        for n in range(VEC_EXITS):
             i, k = divmod(n, NG)
-            u = n + n // 3 + 1
+            u = (XN * n) // 12 + X_AT
             if k % 2 == 0:
                 if n:
-                    put(u - WIDEN_AHEAD, widen_w2, i, k // 2)
+                    sside[u - WIDEN_AHEAD].append((widen_w2, (i, k // 2)))
                 put(u - 1, turn_w2, i, k // 2)
             put(u, exit_w2, i, k)
             if k == NG - 1:
                 batch[4 * (u // 4) + 4].append((quant_w2, (i,)))
+                ready[i] = 4 * (u // 4) + 5
         for p in (2, 3):
-            zside[8 * p - 11].append((turn_y, exit_y, (p,)))
+            zside[8 * p - Y_AT].append((turn_y, exit_y, (p,)))
             batch[8 * p - 8].append((quant_y, (p,)))
-        for half in range(2):
-            put(W3_AT + 2 * half, widen_w2, NI - 1, half)
-            zside[W3_AT + 5 + 2 * half].append((turn_w2, empty_w2, (NI - 1, half)))
-        batch[20].append((quant_w2, (NI - 1,)))
+        for half in range((VEC_EXITS - 12) // 2, 2):
+            sside[W3_AT + 2 * half].append((widen_w2, (NI - 1, half)))
+            zside[W3_AT + X3 + 2 * half].append((turn_w2, empty_w2, (NI - 1, half)))
+        if VEC_EXITS < 16:
+            batch[Q3].append((quant_w2, (NI - 1,)))
         for i in range(NI):
-            u = 17 + 4 * (i // 2) + i % 2
+            u = max(A_AT + 4 * (i // 2) + i % 2, ready[i])
             put(u, contract_blocks, vring, 0, [i])
             put(u + FIN, finish, 0, i)
         for pair in range(2):
             put(B_AT + pair, contract_blocks, vring, 1, [2 * pair, 2 * pair + 1])
         put(B_AT + 1, finish, 1, 0)
         put(B_AT + 2, finish, 1, 1)
-        put(29, contract_blocks, vring, 2, range(NI))
-        put(30, finish, 1, 2)
-        put(30, quant_h, 7, 512, 1536)
+        put(C_AT, contract_blocks, vring, 2, range(NI))
+        put(B2_AT, finish, 1, 2)
+        if B3_AT < 32:
+            put(B3_AT, finish, 1, 3)
+        for i in range(C_EARLY):
+            put(30, finish, 2, i)
+        put(30, quant_h, 28, 2)
         for pair in range(2):
             put(30, open_acc, zring, 3, [2 * pair, 2 * pair + 1])
-        put(30, contract_pass, 3, 1, True, False)
-        put(30, contract_pass, 3, 2, False, False)
+        put(30, contract_pass, 3, 0, True, False)
+        put(30, contract_pass, 3, 1, False, False)
+
+        def vector_slot(u):
+            if u in batch:
+                for fn, fargs in batch[u]:
+                    fn(*fargs)
+                quant_h(u - 4, 2)
+                quant_h(u - 2, 2)
+            gain(u)
+            for fn, fargs in side[u]:
+                fn(*fargs)
 
         jobs = []
         for u in range(32):
@@ -328,8 +369,8 @@ def tile_convnext_pointwise_pair_d7_kernel(
         held = {j: jobs[j][0](*jobs[j][2]) for j in range(ZRING - 1)}
         nc.tensor.matmul(g_ps[:], lhsT=ident16[:], rhs=g_sb[:], start=True, stop=True)
         lay_w1(2, 1)
-        lay_w1(3, 0)
-        lay_w1(3, 1)
+        for jb in range(4 - S_LAY):
+            interleave_w1(3, jb)
         quant_w1(2)
         quant_w1(3)
         for j, (fill, empty, args) in enumerate(jobs):
@@ -339,25 +380,21 @@ def tile_convnext_pointwise_pair_d7_kernel(
             if fill is not expand:
                 continue
             u = args[0]
-            if u in batch:
-                q = u // 4 - 1
-                quant_h(q, pool_cols(q), 1024)
-                quant_h(q, 1024, 1536)
-                for fn, fargs in batch[u]:
-                    fn(*fargs)
-                quant_h(q, 1536, 2048)
-                quant_h(q, 0, 512)
-                quant_h(q, 512, pool_cols(q))
-            gain(u)
-            for fn, fargs in side[u]:
+            for fn, fargs in sside[u]:
                 fn(*fargs)
+            if u >= LAG:
+                vector_slot(u - LAG)
+        for u in range(32 - LAG, 32):
+            vector_slot(u)
 
-        quant_h(7, 0, 512)
-        contract_pass(3, 0, False, False)
-        finish(1, 3)
-        quant_h(7, 1536, 2048)
-        contract_pass(3, NG - 1, False, True)
-        for i in range(NI):
+        quant_h(30, 1)
+        contract_pass(3, 2, False, False)
+        finish(2, C_EARLY)
+        quant_h(31, 1)
+        contract_pass(3, 3, False, True)
+        if B3_AT == 32:
+            finish(1, 3)
+        for i in range(C_EARLY + 1, NI):
             finish(2, i)
         for i in range(NI):
             finish(3, i)

@@ -275,6 +275,8 @@ def tile_convnext_pointwise_pair_d7_kernel(
         nc.sync.dma_start(out=r_sb[:], in_=r.rearrange("(i p) n -> p i n", p=P))
         nc.sync.dma_start(out=gamma_sb[:, :, 0:1], in_=gamma.rearrange("(i p) -> p i", p=P).unsqueeze(2))
 
+        warm = sb([P, 1], F32, "warm")
+        nc.scalar.activation(out=warm[:], in_=ident[:, 0:1], func=GELU)
         nc.scalar.copy(out=ident16[:], in_=ident[:])
         widen(w1_wide[0], w1_raw[0], 0, 1024)
         nc.vector.tensor_copy(out=w1_wide[0][:, 1024:2048], in_=w1_raw[0][:, 1024:2048].bitcast(FP8))

@@ -16,36 +16,24 @@ COPY = mybir.ActivationFunctionType.Copy
 
 P = 128
 NPOS, C, H = 1024, 512, 2048
-NG = H // 512
-NI = C // P
+PASSES = H // 512
+BLOCKS = C // P
 FLOPS = 2 * NPOS * C * H * 2
 
-ZRING = 4
-VRING = 3
-POOL_POS = 96
-LAST_POS = 72
-X_AT = 1
-S_EARLY = 0
-XN = 14
-VEC_EXITS = 14
-S_LAY = 1
-B2_AT = 29
-B3_AT = 29
-C_EARLY = 0
-C_AT = 29
-WIDEN_AHEAD = 2
-FIN = 2
-A_AT = 17
-LAG = 0
-Y_AT = 10
-X3 = 5
-Q3 = 20
-B_AT = 26
-STORE = (1, 1, 1, 1)
-W3_AT = 11
-
 CHUNKS = ((0, 4), (4, 2), (6, 1), (7, 1))
-UNITS = [(k, b0 + b) for b0, nb in CHUNKS for k in range(NG) for b in range(nb)]
+LAST = len(CHUNKS) - 1
+UNITS = [(k, b0 + b) for b0, nb in CHUNKS for k in range(PASSES) for b in range(nb)]
+NUNITS = len(UNITS)
+
+SCALAR_BANKS = 4
+VECTOR_BANKS = 3
+
+POOL_POS = 104
+POOL_POS_LAST = 64
+VECTOR_EXITS = 14
+SCALAR_LAYS = 1
+EXIT_UNITS, EXIT_COPIES = 7, 6
+GAP = 2
 
 
 def tile_convnext_pointwise_pair_d7_kernel(
@@ -54,55 +42,58 @@ def tile_convnext_pointwise_pair_d7_kernel(
     nc = tc.nc
     with ExitStack() as ctx:
         keep = ctx.enter_context(tc.tile_pool(name="keep", bufs=1))
-        gelp = ctx.enter_context(tc.tile_pool(name="gelp", bufs=3))
-        hp = ctx.enter_context(tc.tile_pool(name="hp", bufs=2))
-        zring = ctx.enter_context(tc.psum_pool(name="zring", bufs=ZRING))
-        vring = ctx.enter_context(tc.psum_pool(name="vring", bufs=VRING))
-        gpool = ctx.enter_context(tc.psum_pool(name="gpool", bufs=1))
+        gelu_pool = ctx.enter_context(tc.tile_pool(name="gelu_pool", bufs=3))
+        h_pool = ctx.enter_context(tc.tile_pool(name="h_pool", bufs=2))
+        scalar_banks = ctx.enter_context(tc.psum_pool(name="scalar_banks", bufs=SCALAR_BANKS))
+        vector_banks = ctx.enter_context(tc.psum_pool(name="vector_banks", bufs=VECTOR_BANKS))
+        g_bank = ctx.enter_context(tc.psum_pool(name="g_bank", bufs=1))
         ctx.enter_context(tc.manual_schedule())
 
         def sb(shape, dt, name):
             return keep.tile(shape, dt, name=name, align_bytes=64)
 
+        def shared_tile(shape):
+            return h_pool.tile(shape, BF16, name="shared", bufs=1, align_bytes=64)
+
         ident = sb([P, P], F32, "ident")
         ident16 = sb([P, P], BF16, "ident16")
-        g_ps = gpool.tile([P, 16], F32, name="g_ps")
+        g_ps = g_bank.tile([P, 4 * PASSES], F32, name="g_ps")
         w1s = sb([P, 16], F32, "w1s")
         w2s = sb([P, 64], F32, "w2s")
-        g_sb = sb([P, 16], BF16, "g_sb")
-        gamma_sb = sb([P, 4, 2], BF16, "gamma_sb")
-        y_sb = [sb([P, 2, C], BF16, "y_sb%d" % p) for p in range(4)]
-        y_grp = [sb([P, 1024], BF16, "y_grp%d" % p) for p in range(4)]
+        g_sb = sb([P, 4 * PASSES], BF16, "g_sb")
+        gamma_sb = sb([P, BLOCKS, 2], BF16, "gamma_sb")
+        y_sb = [sb([P, 2, C], BF16, "y_sb%d" % j) for j in range(4)]
+        y_laid = [sb([P, 1024], BF16, "y_laid%d" % j) for j in range(4)]
         y_codes = sb([P, NPOS], U32, "y_codes")
         y_scl = sb([P, NPOS], U8, "y_scl")
-        w1_raw = [sb([P, 2048], U8, "w1_raw%d" % k) for k in range(NG)]
-        w1_wide = [sb([P, 2048], BF16, "w1_wide%d" % k) for k in range(NG)]
-        w1_grp = {k: sb([P, 2048], BF16, "w1_grp%d" % k) for k in (0, 1, 3)}
-        w1_grp[2] = hp.tile([P, 2048], BF16, name="pool_h", bufs=1, align_bytes=64)
-        w1_codes = [sb([P, 512], U32, "w1_codes%d" % k) for k in range(NG)]
-        w1_scl = [sb([P, 512], U8, "w1_scl%d" % k) for k in range(NG)]
-        w2_raw = [sb([P, 2048], U8, "w2_raw%d" % i) for i in range(NI)]
-        w2_wide = [sb([P, 2048], BF16, "w2_wide%d" % i) for i in range(NI)]
-        w2_grp = [sb([P, 2048], BF16, "w2_grp%d" % i) for i in range(NI)]
-        w2_codes = [sb([P, 512], U32, "w2_codes%d" % i) for i in range(NI)]
-        w2_scl = [sb([P, 512], U8, "w2_scl%d" % i) for i in range(NI)]
-        h_codes = [sb([P, 512], U32, "h_codes%d" % q) for q in range(8)]
-        h_scl = [sb([P, 512], U8, "h_scl%d" % q) for q in range(8)]
-        r_sb = sb([P, NI, NPOS], BF16, "r_sb")
-        o_sb = [sb([P, NI, P * nb], F32, "o_sb%d" % c) for c, (b0, nb) in enumerate(CHUNKS)]
+        w1_raw = [sb([P, 2048], U8, "w1_raw%d" % k) for k in range(PASSES)]
+        w1_wide = [sb([P, 2048], BF16, "w1_wide%d" % k) for k in range(PASSES)]
+        w1_laid = {k: sb([P, 2048], BF16, "w1_laid%d" % k) for k in (0, 1, 3)}
+        w1_laid[2] = shared_tile([P, 2048])
+        w1_codes = [sb([P, 512], U32, "w1_codes%d" % k) for k in range(PASSES)]
+        w1_scl = [sb([P, 512], U8, "w1_scl%d" % k) for k in range(PASSES)]
+        w2_raw = [sb([P, 2048], U8, "w2_raw%d" % i) for i in range(BLOCKS)]
+        w2_wide = [sb([P, 2048], BF16, "w2_wide%d" % i) for i in range(BLOCKS)]
+        w2_laid = [sb([P, 2048], BF16, "w2_laid%d" % i) for i in range(BLOCKS)]
+        w2_codes = [sb([P, 512], U32, "w2_codes%d" % i) for i in range(BLOCKS)]
+        w2_scl = [sb([P, 512], U8, "w2_scl%d" % i) for i in range(BLOCKS)]
+        h_codes = [sb([P, 512], U32, "h_codes%d" % q) for q in range(NUNITS // 4)]
+        h_scl = [sb([P, 512], U8, "h_scl%d" % q) for q in range(NUNITS // 4)]
+        r_sb = sb([P, BLOCKS, NPOS], BF16, "r_sb")
+        o_sb = [sb([P, BLOCKS, P * nb], F32, "o_sb%d" % c) for c, (b0, nb) in enumerate(CHUNKS)]
 
-        gel = {}
-        hbf = {}
+        gelus = {}
+        h_laid = {}
+        w2_turned = {}
         acc = {}
-        turned = {}
 
         def load_w1(k):
             src = w1_bytes.rearrange("(p t) n -> p t n", t=4)[:, :, 512 * k : 512 * (k + 1)]
             nc.sync.dma_start(out=w1_raw[k][:].rearrange("p (t n) -> p t n", t=4), in_=src)
 
-        def load_y(p):
+        def load_y(j):
             nc.sync.dma_start(
-                out=y_sb[p][:], in_=y[256 * p : 256 * (p + 1), :].rearrange("(a p) k -> p a k", p=P)
+                out=y_sb[j][:], in_=y[256 * j : 256 * (j + 1), :].rearrange("(p a) k -> p a k", p=P)
             )
 
         def load_w2(i):
@@ -111,70 +102,70 @@ def tile_convnext_pointwise_pair_d7_kernel(
         def widen(dst, src, lo, hi):
             nc.scalar.copy(out=dst[:, lo:hi], in_=src[:, lo:hi].bitcast(FP8))
 
-        def interleave_w1(k, jb):
-            o = w1_grp[k][:].rearrange("p (t m j) -> p m j t", t=4, j=4)[:, 32 * jb : 32 * (jb + 1)]
-            i = w1_wide[k][:].rearrange("p (j m t) -> p m j t", j=4, t=4)[:, 32 * jb : 32 * (jb + 1)]
-            col = w1s[:, 4 * k + jb : 4 * k + jb + 1]
-            if 4 * k + jb >= 16 - S_LAY or (k == 1 and jb == 3 and S_EARLY):
-                nc.scalar.activation(out=o, in_=i, func=COPY, scale=col)
+        def lay_w1(k, b):
+            dst = w1_laid[k][:].rearrange("p (s m t) -> p m t s", s=4, t=4)[:, 32 * b : 32 * (b + 1)]
+            src = w1_wide[k][:].rearrange("p (t m s) -> p m t s", t=4, s=4)[:, 32 * b : 32 * (b + 1)]
+            col = w1s[:, 4 * k + b : 4 * k + b + 1]
+            if 4 * k + b >= 16 - SCALAR_LAYS:
+                nc.scalar.activation(out=dst, in_=src, func=COPY, scale=col)
             else:
-                nc.vector.tensor_scalar(out=o, in0=i, scalar1=col, scalar2=None, op0=MULT)
+                nc.vector.tensor_scalar(out=dst, in0=src, scalar1=col, scalar2=None, op0=MULT)
 
-        def quant(codes, scl, lo, hi, src):
+        def quantise(codes, scl, lo, hi, src):
             nc.vector.quantize_mx(out=codes[:, lo:hi].bitcast(FP8X4), scales=scl[:, lo:hi], in_=src)
 
-        def quant_w1(k):
-            quant(w1_codes[k], w1_scl[k], 0, 512, w1_grp[k][:])
+        def quantise_w1(k):
+            quantise(w1_codes[k], w1_scl[k], 0, 512, w1_laid[k][:])
 
-        def quant_w2(i):
-            quant(w2_codes[i], w2_scl[i], 0, 512, w2_grp[i][:])
+        def quantise_w2(i):
+            quantise(w2_codes[i], w2_scl[i], 0, 512, w2_laid[i][:])
 
-        def quant_y(p):
-            quant(y_codes, y_scl, 256 * p, 256 * (p + 1), y_grp[p][:])
-
-        def lay_w1(k, half):
-            interleave_w1(k, 2 * half)
-            interleave_w1(k, 2 * half + 1)
+        def quantise_y(j):
+            quantise(y_codes, y_scl, 256 * j, 256 * (j + 1), y_laid[j][:])
 
         def turn(pool, words):
-            t = pool.tile([P, 2, 2, P], F32, name="bank")
+            bank = pool.tile([P, 2, 2, P], F32, name="bank")
             for a in range(2):
                 for u in range(2):
-                    nc.tensor.transpose(t[:, a, u, :], words[:, 256 * a + u : 256 * (a + 1) : 2], ident[:])
-            return t
+                    nc.tensor.transpose(bank[:, a, u, :], words[:, 256 * a + u : 256 * (a + 1) : 2], ident[:])
+            return bank
 
-        def turn_y(p):
-            return turn(zring, y_sb[p][:].rearrange("p a k -> p (a k)").bitcast(F32))
+        def turn_y(j):
+            return turn(scalar_banks, y_sb[j][:].rearrange("p a k -> p (a k)").bitcast(F32))
 
-        def exit_y(t, p):
-            o = y_grp[p][:].bitcast(F32).rearrange("p (a r u) -> p a r u", a=2, u=2)
-            nc.scalar.copy(out=o, in_=t[:].rearrange("p a u r -> p a r u"))
+        def exit_y(bank, j):
+            dst = y_laid[j][:].bitcast(F32).rearrange("p (n a u) -> p n a u", a=2, u=2)
+            nc.scalar.copy(out=dst, in_=bank[:].rearrange("p a u n -> p n a u"))
 
         def widen_w2(i, half):
             widen(w2_wide[i], w2_raw[i], 1024 * half, 1024 * (half + 1))
 
         def turn_w2(i, half):
-            pool = zring if NG * i + 2 * half >= VEC_EXITS else vring
-            turned["w2", i, half] = turn(pool, w2_wide[i][:, 1024 * half : 1024 * (half + 1)].bitcast(F32))
+            pool = vector_banks if PASSES * i + 2 * half < VECTOR_EXITS else scalar_banks
+            w2_turned[i, half] = turn(pool, w2_wide[i][:, 1024 * half : 1024 * (half + 1)].bitcast(F32))
 
         def exit_w2(i, k):
-            o = w2_grp[i][:, 512 * k : 512 * (k + 1)].rearrange("p (r u e) -> p r u e", u=2, e=2)
-            s = turned["w2", i, k // 2][:, k % 2].rearrange("p u r -> p (u r)").bitcast(BF16)
-            s = s.rearrange("p (u r e) -> p r u e", u=2, e=2)
+            dst = w2_laid[i][:, 512 * k : 512 * (k + 1)].rearrange("p (n u e) -> p n u e", u=2, e=2)
+            src = w2_turned[i, k // 2][:, k % 2].rearrange("p u n -> p (u n)").bitcast(BF16)
+            src = src.rearrange("p (u n e) -> p n u e", u=2, e=2)
             col = w2s[:, 16 * i + 4 * k : 16 * i + 4 * k + 1]
-            if NG * i + k >= VEC_EXITS:
-                nc.scalar.activation(out=o, in_=s, func=COPY, scale=col)
+            if PASSES * i + k < VECTOR_EXITS:
+                nc.vector.tensor_scalar(out=dst, in0=src, scalar1=col, scalar2=None, op0=MULT)
             else:
-                nc.vector.tensor_scalar(out=o, in0=s, scalar1=col, scalar2=None, op0=MULT)
+                nc.scalar.activation(out=dst, in_=src, func=COPY, scale=col)
+
+        def exit_w2_bank(bank, i, half):
+            exit_w2(i, 2 * half)
+            exit_w2(i, 2 * half + 1)
 
         def expand(u):
             k, b = UNITS[u]
-            z = zring.tile([P, 4, P], F32, name="bank")
-            for t in range(4):
+            z = scalar_banks.tile([P, 4, P], F32, name="bank")
+            for s in range(4):
                 nc.tensor.matmul_mx(
-                    out=z[:, t, :],
-                    lhsT=w1_codes[k][:, P * t : P * (t + 1)].bitcast(FP8X4),
-                    lhsT_scale=w1_scl[k][:, P * t : P * (t + 1)],
+                    out=z[:, s, :],
+                    lhsT=w1_codes[k][:, P * s : P * (s + 1)].bitcast(FP8X4),
+                    lhsT_scale=w1_scl[k][:, P * s : P * (s + 1)],
                     rhs=y_codes[:, P * b : P * (b + 1)].bitcast(FP8X4),
                     rhs_scale=y_scl[:, P * b : P * (b + 1)],
                     start=True,
@@ -184,39 +175,38 @@ def tile_convnext_pointwise_pair_d7_kernel(
 
         def gelu(z, u):
             if u % 4 == 0:
-                gel[u // 4] = gelp.tile([P, 2048], F32, name="gel")
-            a = gel[u // 4][:, 512 * (u % 4) : 512 * (u % 4 + 1)]
-            nc.scalar.activation(out=a.rearrange("p (n t) -> p n t", t=4), in_=z[:].rearrange("p t n -> p n t"), func=GELU)
+                gelus[u // 4] = gelu_pool.tile([P, 4, P, 4], F32, name="gelus")
+            nc.scalar.activation(out=gelus[u // 4][:, u % 4], in_=z[:].rearrange("p s n -> p n s"), func=GELU)
 
-        def gain_of(gt, u, n, npos):
+        def gain_part(eng, g_tile, dst, u, n, lo, hi):
             k0, k1 = UNITS[u][0], UNITS[u + n - 1][0]
-            gk = gt[:, 4 * k0 : 4 * (k1 + 1)].rearrange("p (k t) -> p k t", t=4)
-            return gk.unsqueeze(2).to_broadcast([P, n, npos, 4])
-
-        def gain_part(eng, gt, dst, u, n, lo, hi):
-            a = gel[u // 4][:].rearrange("p (u n t) -> p u n t", u=4, t=4)[:, u % 4 : u % 4 + n, lo:hi]
-            eng.tensor_tensor(out=dst[:, :, lo:hi], in0=a, in1=gain_of(gt, u, n, hi - lo), op=MULT)
+            g_part = g_tile[:, 4 * k0 : 4 * (k1 + 1)].rearrange("p (k t) -> p k t", t=4)
+            eng.tensor_tensor(
+                out=dst[:, :, lo:hi],
+                in0=gelus[u // 4][:, u % 4 : u % 4 + n, lo:hi],
+                in1=g_part.unsqueeze(2).to_broadcast([P, n, hi - lo, 4]),
+                op=MULT,
+            )
 
         def gain(u):
             if u % 4 == 1:
-                hbf[u - 1] = hp.tile([P, 2, P, 4], BF16, name="pool_h", bufs=1, align_bytes=64)
-                cut = LAST_POS if u > 28 else POOL_POS
-                gain_part(nc.gpsimd, g_sb, hbf[u - 1], u - 1, 2, 0, cut)
-                gain_part(nc.vector, g_ps, hbf[u - 1], u - 1, 2, cut, P)
+                h_laid[u - 1] = shared_tile([P, 2, P, 4])
+                cut = POOL_POS_LAST if u > NUNITS - 4 else POOL_POS
+                gain_part(nc.gpsimd, g_sb, h_laid[u - 1], u - 1, 2, 0, cut)
+                gain_part(nc.vector, g_ps, h_laid[u - 1], u - 1, 2, cut, P)
             elif u % 4 > 1:
                 if u % 4 == 2:
-                    hbf[u] = hp.tile([P, 2, P, 4], BF16, name="vec_h", align_bytes=64)
-                dst = hbf[u - u % 2][:, u % 2 : u % 2 + 1]
-                gain_part(nc.vector, g_ps, dst, u, 1, 0, P)
+                    h_laid[u] = h_pool.tile([P, 2, P, 4], BF16, name="vector_h", align_bytes=64)
+                gain_part(nc.vector, g_ps, h_laid[u - u % 2][:, u % 2 : u % 2 + 1], u, 1, 0, P)
 
-        def quant_h(u, n):
-            src = hbf[u - u % 2][:, u % 2 : u % 2 + n].rearrange("p u n t -> p (u n t)")
-            quant(h_codes[u // 4], h_scl[u // 4], P * (u % 4), P * (u % 4 + n), src)
+        def quantise_h(u, n):
+            src = h_laid[u - u % 2][:, u % 2 : u % 2 + n].rearrange("p u n t -> p (u n t)")
+            quantise(h_codes[u // 4], h_scl[u // 4], P * (u % 4), P * (u % 4 + n), src)
 
-        def open_acc(pool, c, blocks):
-            t = pool.tile([P, len(blocks), P * CHUNKS[c][1]], F32, name="bank")
+        def open_sums(pool, c, blocks):
+            bank = pool.tile([P, len(blocks), P * CHUNKS[c][1]], F32, name="bank")
             for n, i in enumerate(blocks):
-                acc[c, i] = t[:, n, :]
+                acc[c, i] = bank[:, n, :]
 
         def contract(c, i, k, start, stop):
             b0, nb = CHUNKS[c]
@@ -232,15 +222,15 @@ def tile_convnext_pointwise_pair_d7_kernel(
                 stop=stop,
             )
 
-        def contract_blocks(pool, c, blocks):
-            open_acc(pool, c, blocks)
+        def contract_bank(c, blocks):
+            open_sums(vector_banks, c, blocks)
             for i in blocks:
-                for k in range(NG):
-                    contract(c, i, k, k == 0, k == NG - 1)
+                for k in range(PASSES):
+                    contract(c, i, k, k == 0, k == PASSES - 1)
 
-        def contract_pass(c, k, first, last):
-            for i in range(NI):
-                contract(c, i, k, first and i % 2 == 0, last and i % 2 == 1)
+        def contract_last(k):
+            for i in range(BLOCKS):
+                contract(LAST, i, k, k == 0 and i % 2 == 0, k == PASSES - 1 and i % 2 == 1)
 
         def finish(c, i):
             b0, nb = CHUNKS[c]
@@ -248,10 +238,7 @@ def tile_convnext_pointwise_pair_d7_kernel(
             nc.vector.scalar_tensor_tensor(
                 out=o_sb[c][:, i, :], in0=acc[c, i], scalar=gamma_sb[:, i, 0:1], in1=r_sb[:, i, cols], op0=MULT, op1=ADD
             )
-            n = STORE[c]
-            if i % n == n - 1:
-                rows = out[P * (i + 1 - n) : P * (i + 1), cols].rearrange("(i p) n -> p i n", p=P)
-                nc.sync.dma_start(out=rows, in_=o_sb[c][:, i + 1 - n : i + 1, :])
+            nc.sync.dma_start(out=out[P * i : P * (i + 1), cols], in_=o_sb[c][:, i, :])
 
         load_w1(0)
         load_w1(1)
@@ -280,123 +267,98 @@ def tile_convnext_pointwise_pair_d7_kernel(
         nc.scalar.copy(out=ident16[:], in_=ident[:])
         widen(w1_wide[0], w1_raw[0], 0, 1024)
         nc.vector.tensor_copy(out=w1_wide[0][:, 1024:2048], in_=w1_raw[0][:, 1024:2048].bitcast(FP8))
-        for k in range(1, NG):
+        for k in range(1, PASSES):
             widen(w1_wide[k], w1_raw[k], 0, 2048)
-            if k == 1 and S_EARLY:
-                interleave_w1(1, 3)
-        ty = [turn_y(0), turn_y(1)]
-        exit_y(ty[0], 0)
-        exit_y(ty[1], 1)
-        for jb in range(4 - S_LAY, 4):
-            interleave_w1(3, jb)
+        y_banks = [turn_y(0), turn_y(1)]
+        exit_y(y_banks[0], 0)
+        exit_y(y_banks[1], 1)
+        for n in range(16 - SCALAR_LAYS, 16):
+            lay_w1(*divmod(n, 4))
         widen_w2(0, 0)
-        lay_w1(0, 0)
-        lay_w1(0, 1)
-        lay_w1(1, 0)
-        quant_w1(0)
-        interleave_w1(1, 2)
-        if not S_EARLY:
-            interleave_w1(1, 3)
-        lay_w1(2, 0)
-        quant_y(0)
-        quant_w1(1)
-        quant_y(1)
+        for n in range(0, 6):
+            lay_w1(*divmod(n, 4))
+        quantise_w1(0)
+        for n in range(6, 10):
+            lay_w1(*divmod(n, 4))
+        quantise_y(0)
+        quantise_w1(1)
+        quantise_y(1)
 
-        side = {u: [] for u in range(32)}
-        zside = {u: [] for u in range(32)}
-        sside = {u: [] for u in range(32)}
-        batch = {u: [] for u in range(4, 32, 4)}
+        scalar_side = {u: [] for u in range(NUNITS)}
+        bank_side = {u: [] for u in range(NUNITS)}
+        vector_side = {u: [] for u in range(NUNITS)}
+        runs = {u: [] for u in range(4, NUNITS, 4)}
 
         def put(u, fn, *args):
-            side[u].append((fn, args))
+            vector_side[u].append((fn, args))
 
-        def empty_w2(t, i, half):
-            exit_w2(i, 2 * half)
-            exit_w2(i, 2 * half + 1)
-
-        ready = [Q3 + 1] * NI
-        for n in range(VEC_EXITS):
-            i, k = divmod(n, NG)
-            u = (XN * n) // 12 + X_AT
+        for n in range(VECTOR_EXITS):
+            i, k = divmod(n, PASSES)
+            u = EXIT_UNITS * n // EXIT_COPIES + 1
             if k % 2 == 0:
                 if n:
-                    sside[u - WIDEN_AHEAD].append((widen_w2, (i, k // 2)))
+                    scalar_side[u - GAP].append((widen_w2, (i, k // 2)))
                 put(u - 1, turn_w2, i, k // 2)
             put(u, exit_w2, i, k)
-            if k == NG - 1:
-                batch[4 * (u // 4) + 4].append((quant_w2, (i,)))
-                ready[i] = 4 * (u // 4) + 5
-        for p in (2, 3):
-            zside[8 * p - Y_AT].append((turn_y, exit_y, (p,)))
-            batch[8 * p - 8].append((quant_y, (p,)))
-        for half in range((VEC_EXITS - 12) // 2, 2):
-            sside[W3_AT + 2 * half].append((widen_w2, (NI - 1, half)))
-            zside[W3_AT + X3 + 2 * half].append((turn_w2, empty_w2, (NI - 1, half)))
-        if VEC_EXITS < 16:
-            batch[Q3].append((quant_w2, (NI - 1,)))
-        for i in range(NI):
-            u = max(A_AT + 4 * (i // 2) + i % 2, ready[i])
-            put(u, contract_blocks, vring, 0, [i])
-            put(u + FIN, finish, 0, i)
+            if k == PASSES - 1:
+                runs[4 * (u // 4) + 4].append((quantise_w2, (i,)))
+        for j in (2, 3):
+            bank_side[8 * j - 8 - GAP].append((turn_y, exit_y, (j,)))
+            runs[8 * j - 8].append((quantise_y, (j,)))
+        banks = [(c, range(i, i + 4 // nb)) for c, (b0, nb) in enumerate(CHUNKS[:LAST]) for i in range(0, BLOCKS, 4 // nb)]
+        first = PASSES * CHUNKS[0][1]
+        for n, (c, blocks) in enumerate(banks):
+            u = first + 4 * (n // 2) + n % 2 + 1
+            put(u, contract_bank, c, blocks)
+            if c < LAST - 1:
+                for i in blocks:
+                    put(u + GAP, finish, c, i)
+        u = first + 4 - GAP
+        scalar_side[u - (SCALAR_BANKS - 1) - GAP].append((widen_w2, (BLOCKS - 1, 1)))
+        bank_side[u].append((turn_w2, exit_w2_bank, (BLOCKS - 1, 1)))
+        runs[first + 4].append((quantise_w2, (BLOCKS - 1,)))
+        put(NUNITS - 2, quantise_h, NUNITS - 4, 2)
         for pair in range(2):
-            put(B_AT + pair, contract_blocks, vring, 1, [2 * pair, 2 * pair + 1])
-        put(B_AT + 1, finish, 1, 0)
-        put(B_AT + 2, finish, 1, 1)
-        put(C_AT, contract_blocks, vring, 2, range(NI))
-        put(B2_AT, finish, 1, 2)
-        if B3_AT < 32:
-            put(B3_AT, finish, 1, 3)
-        for i in range(C_EARLY):
-            put(30, finish, 2, i)
-        put(30, quant_h, 28, 2)
-        for pair in range(2):
-            put(30, open_acc, zring, 3, [2 * pair, 2 * pair + 1])
-        put(30, contract_pass, 3, 0, True, False)
-        put(30, contract_pass, 3, 1, False, False)
+            put(NUNITS - 2, open_sums, scalar_banks, LAST, [2 * pair, 2 * pair + 1])
+        put(NUNITS - 2, contract_last, 0)
+        put(NUNITS - 2, contract_last, 1)
 
-        def vector_slot(u):
-            if u in batch:
-                for fn, fargs in batch[u]:
-                    fn(*fargs)
-                quant_h(u - 4, 2)
-                quant_h(u - 2, 2)
-            gain(u)
-            for fn, fargs in side[u]:
-                fn(*fargs)
-
-        jobs = []
-        for u in range(32):
-            jobs.append((expand, gelu, (u,)))
-            jobs.extend(zside[u])
-        held = {j: jobs[j][0](*jobs[j][2]) for j in range(ZRING - 1)}
+        steps = []
+        for u in range(NUNITS):
+            steps.append((expand, gelu, (u,)))
+            steps.extend(bank_side[u])
+        ahead = SCALAR_BANKS - 1
+        filled = {j: steps[j][0](*steps[j][2]) for j in range(ahead)}
         nc.tensor.matmul(g_ps[:], lhsT=ident16[:], rhs=g_sb[:], start=True, stop=True)
-        lay_w1(2, 1)
-        for jb in range(4 - S_LAY):
-            interleave_w1(3, jb)
-        quant_w1(2)
-        quant_w1(3)
-        for j, (fill, empty, args) in enumerate(jobs):
-            if j + ZRING - 1 < len(jobs):
-                held[j + ZRING - 1] = jobs[j + ZRING - 1][0](*jobs[j + ZRING - 1][2])
-            empty(held[j], *args)
+        for n in range(10, 16 - SCALAR_LAYS):
+            lay_w1(*divmod(n, 4))
+        quantise_w1(2)
+        quantise_w1(3)
+
+        for j, (fill, empty, args) in enumerate(steps):
+            if j + ahead < len(steps):
+                filled[j + ahead] = steps[j + ahead][0](*steps[j + ahead][2])
+            empty(filled[j], *args)
             if fill is not expand:
                 continue
             u = args[0]
-            for fn, fargs in sside[u]:
-                fn(*fargs)
-            if u >= LAG:
-                vector_slot(u - LAG)
-        for u in range(32 - LAG, 32):
-            vector_slot(u)
+            for fn, fn_args in scalar_side[u]:
+                fn(*fn_args)
+            if u in runs:
+                for fn, fn_args in runs[u]:
+                    fn(*fn_args)
+                quantise_h(u - 4, 2)
+                quantise_h(u - 2, 2)
+            gain(u)
+            for fn, fn_args in vector_side[u]:
+                fn(*fn_args)
 
-        quant_h(30, 1)
-        contract_pass(3, 2, False, False)
-        finish(2, C_EARLY)
-        quant_h(31, 1)
-        contract_pass(3, 3, False, True)
-        if B3_AT == 32:
-            finish(1, 3)
-        for i in range(C_EARLY + 1, NI):
-            finish(2, i)
-        for i in range(NI):
-            finish(3, i)
+        quantise_h(NUNITS - 2, 1)
+        contract_last(PASSES - 2)
+        finish(LAST - 1, 0)
+        quantise_h(NUNITS - 1, 1)
+        contract_last(PASSES - 1)
+        for i in range(1, BLOCKS):
+            finish(LAST - 1, i)
+        for i in range(BLOCKS):
+            finish(LAST, i)

@@ -28,11 +28,11 @@ NUNITS = len(UNITS)
 SCALAR_BANKS = 4
 VECTOR_BANKS = 3
 
-POOL_POS = 104
+POOL_POS = 100
 POOL_POS_LAST = 64
 VECTOR_EXITS = 14
 SCALAR_LAYS = 1
-EXIT_UNITS, EXIT_COPIES = 7, 6
+EXIT_UNITS, EXIT_COPIES = 5, 4
 GAP = 2
 
 
@@ -189,15 +189,18 @@ def tile_convnext_pointwise_pair_d7_kernel(
             )
 
         def gain(u):
+            first_unit = u - u % 4
+            last_group = first_unit == NUNITS - 4
+            cut = POOL_POS_LAST if last_group else POOL_POS
             if u % 4 == 1:
-                h_laid[u - 1] = shared_tile([P, 2, P, 4])
-                cut = POOL_POS_LAST if u > NUNITS - 4 else POOL_POS
-                gain_part(nc.gpsimd, g_sb, h_laid[u - 1], u - 1, 2, 0, cut)
-                gain_part(nc.vector, g_ps, h_laid[u - 1], u - 1, 2, cut, P)
-            elif u % 4 > 1:
-                if u % 4 == 2:
-                    h_laid[u] = h_pool.tile([P, 2, P, 4], BF16, name="vector_h", align_bytes=64)
+                h_laid[first_unit] = shared_tile([P, 2, P, 4])
+                gain_part(nc.gpsimd, g_sb, h_laid[first_unit], first_unit, 2, 0, cut)
+            if u % 4 == 2:
+                h_laid[u] = h_pool.tile([P, 2, P, 4], BF16, name="vector_h", align_bytes=64)
+            if u % 4 > 1:
                 gain_part(nc.vector, g_ps, h_laid[u - u % 2][:, u % 2 : u % 2 + 1], u, 1, 0, P)
+            if u % 4 == (1 if last_group else 2):
+                gain_part(nc.vector, g_ps, h_laid[first_unit], first_unit, 2, cut, P)
 
         def quantise_h(u, n):
             src = h_laid[u - u % 2][:, u % 2 : u % 2 + n].rearrange("p u n t -> p (u n t)")
@@ -303,8 +306,8 @@ def tile_convnext_pointwise_pair_d7_kernel(
             if k == PASSES - 1:
                 runs[4 * (u // 4) + 4].append((quantise_w2, (i,)))
         for j in (2, 3):
-            bank_side[8 * j - 8 - GAP].append((turn_y, exit_y, (j,)))
-            runs[8 * j - 8].append((quantise_y, (j,)))
+            bank_side[8 * j - 12 - GAP].append((turn_y, exit_y, (j,)))
+            runs[8 * j - 12].append((quantise_y, (j,)))
         banks = [(c, range(i, i + 4 // nb)) for c, (b0, nb) in enumerate(CHUNKS[:LAST]) for i in range(0, BLOCKS, 4 // nb)]
         first = PASSES * CHUNKS[0][1]
         for n, (c, blocks) in enumerate(banks):

@@ -265,9 +265,11 @@ def tile_convnext_pointwise_pair_d7_kernel(
         nc.sync.dma_start(out=r_sb[:], in_=r.rearrange("(i p) n -> p i n", p=P))
         nc.sync.dma_start(out=gamma_sb[:, :, 0:1], in_=gamma.rearrange("(i p) -> p i", p=P).unsqueeze(2))
 
+        zero = sb([P, 1], F32, "zero")
         warm = sb([P, 1], F32, "warm")
-        nc.scalar.activation(out=warm[:], in_=ident[:, 0:1], func=GELU)
-        nc.scalar.copy(out=ident16[:], in_=ident[:])
+        nc.vector.memset(zero[:], 0.0)
+        nc.scalar.activation(out=warm[:], in_=zero[:], func=GELU)
+        nc.vector.tensor_copy(out=ident16[:], in_=ident[:])
         widen(w1_wide[0], w1_raw[0], 0, 1024)
         nc.vector.tensor_copy(out=w1_wide[0][:, 1024:2048], in_=w1_raw[0][:, 1024:2048].bitcast(FP8))
         for k in range(1, PASSES):

@@ -243,10 +243,11 @@ def tile_convnext_pointwise_pair_d7_kernel(
             )
             nc.sync.dma_start(out=out[P * i : P * (i + 1), cols], in_=o_sb[c][:, i, :])
 
+        for q in range(4):
+            queue = nc.scalar if q % 2 else nc.sync
+            queue.dma_start(out=w1s[32 * q : 32 * (q + 1), :], in_=w1_scale[q].partition_broadcast(32))
         load_w1(0)
         load_w1(1)
-        for q in range(4):
-            nc.scalar.dma_start(out=w1s[32 * q : 32 * (q + 1), :], in_=w1_scale[q].partition_broadcast(32))
         load_w1(2)
         load_y(0)
         make_identity(nc, ident[:])

@@ -29,7 +29,10 @@ SCALAR_BANKS = 4
 VECTOR_BANKS = 3
 
 POOL_POS = 100
-POOL_POS_LAST = 64
+POOL_POS_LAST = 52
+POOL_LATE, POOL_POS_LATE = 20, 96
+SCALAR_UNITS = (22, 26, 30, 31)
+SCALAR_POS = 48
 VECTOR_EXITS = 14
 SCALAR_LAYS = 1
 EXIT_UNITS, EXIT_COPIES = 5, 4
@@ -61,6 +64,7 @@ def tile_convnext_pointwise_pair_d7_kernel(
         w1s = sb([P, 16], F32, "w1s")
         w2s = sb([P, 64], F32, "w2s")
         g_sb = sb([P, 4 * PASSES], BF16, "g_sb")
+        g32 = sb([P, 4 * PASSES], F32, "g32")
         gamma_sb = sb([P, BLOCKS, 2], BF16, "gamma_sb")
         y_sb = [sb([P, 2, C], BF16, "y_sb%d" % j) for j in range(4)]
         y_laid = [sb([P, 1024], BF16, "y_laid%d" % j) for j in range(4)]
@@ -191,16 +195,27 @@ def tile_convnext_pointwise_pair_d7_kernel(
         def gain(u):
             first_unit = u - u % 4
             last_group = first_unit == NUNITS - 4
-            cut = POOL_POS_LAST if last_group else POOL_POS
+            cut = POOL_POS_LAST if last_group else POOL_POS_LATE if first_unit >= POOL_LATE else POOL_POS
             if u % 4 == 1:
                 h_laid[first_unit] = shared_tile([P, 2, P, 4])
                 gain_part(nc.gpsimd, g_sb, h_laid[first_unit], first_unit, 2, 0, cut)
             if u % 4 == 2:
                 h_laid[u] = h_pool.tile([P, 2, P, 4], BF16, name="vector_h", align_bytes=64)
             if u % 4 > 1:
-                gain_part(nc.vector, g_ps, h_laid[u - u % 2][:, u % 2 : u % 2 + 1], u, 1, 0, P)
+                hi = P - SCALAR_POS if u in SCALAR_UNITS else P
+                gain_part(nc.vector, g_ps, h_laid[u - u % 2][:, u % 2 : u % 2 + 1], u, 1, 0, hi)
             if u % 4 == (1 if last_group else 2):
                 gain_part(nc.vector, g_ps, h_laid[first_unit], first_unit, 2, cut, P)
+
+        def scalar_gain(u):
+            for t in range(4):
+                col = 4 * UNITS[u][0] + t
+                nc.scalar.activation(
+                    out=h_laid[u - u % 2][:, u % 2, P - SCALAR_POS : P, t],
+                    in_=gelus[u // 4][:, u % 4, P - SCALAR_POS : P, t],
+                    func=COPY,
+                    scale=g32[:, col : col + 1],
+                )
 
         def quantise_h(u, n):
             src = h_laid[u - u % 2][:, u % 2 : u % 2 + n].rearrange("p u n t -> p (u n t)")
@@ -298,6 +313,9 @@ def tile_convnext_pointwise_pair_d7_kernel(
         def put(u, fn, *args):
             vector_side[u].append((fn, args))
 
+        scalar_side[SCALAR_UNITS[0] - GAP].append((nc.scalar.copy, (g32[:], g_sb[:])))
+        for u in SCALAR_UNITS:
+            scalar_side[u | 1].append((scalar_gain, (u,)))
         for n in range(VECTOR_EXITS):
             i, k = divmod(n, PASSES)
             u = EXIT_UNITS * n // EXIT_COPIES + 1
@@ -314,7 +332,7 @@ def tile_convnext_pointwise_pair_d7_kernel(
         banks = [(c, range(i, i + 4 // nb)) for c, (b0, nb) in enumerate(CHUNKS[:LAST]) for i in range(0, BLOCKS, 4 // nb)]
         first = PASSES * CHUNKS[0][1]
         for n, (c, blocks) in enumerate(banks):
-            u = first + 4 * (n // 2) + n % 2 + 1
+            u = first + 2 * n + 1
             put(u, contract_bank, c, blocks)
             if c < LAST - 1:
                 for i in blocks:

@@ -29,10 +29,9 @@ SCALAR_BANKS = 4
 VECTOR_BANKS = 3
 
 POOL_POS = 100
-POOL_POS_LAST = 52
-POOL_LATE, POOL_POS_LATE = 20, 96
-SCALAR_UNITS = (22, 26, 30, 31)
-SCALAR_POS = 48
+POOL_POS_LAST = 56
+SCALAR_UNITS = (NUNITS - 10, NUNITS - 6, NUNITS - 2, NUNITS - 1)
+SCALAR_POS = 32
 VECTOR_EXITS = 14
 SCALAR_LAYS = 1
 EXIT_UNITS, EXIT_COPIES = 5, 4
@@ -195,7 +194,7 @@ def tile_convnext_pointwise_pair_d7_kernel(
         def gain(u):
             first_unit = u - u % 4
             last_group = first_unit == NUNITS - 4
-            cut = POOL_POS_LAST if last_group else POOL_POS_LATE if first_unit >= POOL_LATE else POOL_POS
+            cut = POOL_POS_LAST if last_group else POOL_POS
             if u % 4 == 1:
                 h_laid[first_unit] = shared_tile([P, 2, P, 4])
                 gain_part(nc.gpsimd, g_sb, h_laid[first_unit], first_unit, 2, 0, cut)

@@ -69,7 +69,8 @@ def tile_convnext_pointwise_pair_d7_kernel(
         y_laid = [sb([P, 1024], BF16, "y_laid%d" % j) for j in range(4)]
         y_codes = sb([P, NPOS], U32, "y_codes")
         y_scl = sb([P, NPOS], U8, "y_scl")
-        w1_raw = [sb([P, 2048], U8, "w1_raw%d" % k) for k in range(PASSES)]
+        w1_first = [sb([P, 1024], U8, "w1_first%d" % h) for h in range(2)]
+        w1_raw = {k: sb([P, 2048], U8, "w1_raw%d" % k) for k in range(1, PASSES)}
         w1_wide = [sb([P, 2048], BF16, "w1_wide%d" % k) for k in range(PASSES)]
         w1_laid = {k: sb([P, 2048], BF16, "w1_laid%d" % k) for k in (0, 1, 3)}
         w1_laid[2] = shared_tile([P, 2048])
@@ -93,6 +94,10 @@ def tile_convnext_pointwise_pair_d7_kernel(
         def load_w1(k):
             src = w1_bytes.rearrange("(p t) n -> p t n", t=4)[:, :, 512 * k : 512 * (k + 1)]
             nc.sync.dma_start(out=w1_raw[k][:].rearrange("p (t n) -> p t n", t=4), in_=src)
+
+        def load_w1_half(h):
+            src = w1_bytes.rearrange("(p t) n -> p t n", t=4)[:, 2 * h : 2 * h + 2, 0:512]
+            nc.sync.dma_start(out=w1_first[h][:].rearrange("p (t n) -> p t n", t=2), in_=src)
 
         def load_y(j):
             nc.sync.dma_start(
@@ -255,12 +260,14 @@ def tile_convnext_pointwise_pair_d7_kernel(
             nc.vector.scalar_tensor_tensor(
                 out=o_sb[c][:, i, :], in0=acc[c, i], scalar=gamma_sb[:, i, 0:1], in1=r_sb[:, i, cols], op0=MULT, op1=ADD
             )
-            nc.sync.dma_start(out=out[P * i : P * (i + 1), cols], in_=o_sb[c][:, i, :])
+            queue = nc.scalar if c == LAST and i % 2 else nc.sync
+            queue.dma_start(out=out[P * i : P * (i + 1), cols], in_=o_sb[c][:, i, :])
 
         for q in range(4):
             queue = nc.scalar if q % 2 else nc.sync
             queue.dma_start(out=w1s[32 * q : 32 * (q + 1), :], in_=w1_scale[q].partition_broadcast(32))
-        load_w1(0)
+        load_w1_half(0)
+        load_w1_half(1)
         load_w1(1)
         load_w1(2)
         load_y(0)
@@ -285,8 +292,11 @@ def tile_convnext_pointwise_pair_d7_kernel(
         nc.vector.memset(zero[:], 0.0)
         nc.scalar.activation(out=warm[:], in_=zero[:], func=GELU)
         nc.vector.tensor_copy(out=ident16[:], in_=ident[:])
-        widen(w1_wide[0], w1_raw[0], 0, 1024)
-        nc.vector.tensor_copy(out=w1_wide[0][:, 1024:2048], in_=w1_raw[0][:, 1024:2048].bitcast(FP8))
+        for h in range(2):
+            nc.scalar.copy(out=w1_wide[0][:, 1024 * h : 1024 * h + 512], in_=w1_first[h][:, 0:512].bitcast(FP8))
+            nc.vector.tensor_copy(
+                out=w1_wide[0][:, 1024 * h + 512 : 1024 * (h + 1)], in_=w1_first[h][:, 512:1024].bitcast(FP8)
+            )
         for k in range(1, PASSES):
             widen(w1_wide[k], w1_raw[k], 0, 2048)
         y_banks = [turn_y(0), turn_y(1)]

@@ -117,6 +117,7 @@ def tile_convnext_pointwise_pair_d7_kernel(
             if 4 * k + b >= 16 - SCALAR_LAYS:
                 nc.scalar.activation(out=dst, in_=src, func=COPY, scale=col)
             else:
+                dst, src = dst.rearrange("p m t s -> p m s t"), src.rearrange("p m t s -> p m s t")
                 nc.vector.tensor_scalar(out=dst, in0=src, scalar1=col, scalar2=None, op0=MULT)
 
         def quantise(codes, scl, lo, hi, src):

@@ -33,7 +33,7 @@ POOL_POS_LAST = 56
 SCALAR_UNITS = (NUNITS - 10, NUNITS - 6, NUNITS - 2, NUNITS - 1)
 SCALAR_POS = 32
 VECTOR_EXITS = 14
-SCALAR_LAYS = 1
+SCALAR_LAYS = 0
 EXIT_UNITS, EXIT_COPIES = 5, 4
 GAP = 2
 
@@ -71,7 +71,7 @@ def tile_convnext_pointwise_pair_d7_kernel(
         y_scl = sb([P, NPOS], U8, "y_scl")
         w1_first = [sb([P, 1024], U8, "w1_first%d" % h) for h in range(2)]
         w1_raw = {k: sb([P, 2048], U8, "w1_raw%d" % k) for k in range(1, PASSES)}
-        w1_wide = [sb([P, 2048], BF16, "w1_wide%d" % k) for k in range(PASSES)]
+        w1_wide = [sb([P, 2048], BF16, "w1_wide%d" % k) for k in range(1)]
         w1_laid = {k: sb([P, 2048], BF16, "w1_laid%d" % k) for k in (0, 1, 3)}
         w1_laid[2] = shared_tile([P, 2048])
         w1_codes = [sb([P, 512], U32, "w1_codes%d" % k) for k in range(PASSES)]
@@ -112,7 +112,7 @@ def tile_convnext_pointwise_pair_d7_kernel(
 
         def lay_w1(k, b):
             dst = w1_laid[k][:].rearrange("p (s m t) -> p m t s", s=4, t=4)[:, 32 * b : 32 * (b + 1)]
-            src = w1_wide[k][:].rearrange("p (t m s) -> p m t s", t=4, s=4)[:, 32 * b : 32 * (b + 1)]
+            src = (w1_wide[0][:] if k == 0 else w1_raw[k][:].bitcast(FP8)).rearrange("p (t m s) -> p m t s", t=4, s=4)[:, 32 * b : 32 * (b + 1)]
             col = w1s[:, 4 * k + b : 4 * k + b + 1]
             if 4 * k + b >= 16 - SCALAR_LAYS:
                 nc.scalar.activation(out=dst, in_=src, func=COPY, scale=col)
@@ -298,8 +298,6 @@ def tile_convnext_pointwise_pair_d7_kernel(
             nc.vector.tensor_copy(
                 out=w1_wide[0][:, 1024 * h + 512 : 1024 * (h + 1)], in_=w1_first[h][:, 512:1024].bitcast(FP8)
             )
-        for k in range(1, PASSES):
-            widen(w1_wide[k], w1_raw[k], 0, 2048)
         y_banks = [turn_y(0), turn_y(1)]
         exit_y(y_banks[0], 0)
         exit_y(y_banks[1], 1)

@@ -33,7 +33,6 @@ POOL_POS_LAST = 56
 SCALAR_UNITS = (NUNITS - 10, NUNITS - 6, NUNITS - 2, NUNITS - 1)
 SCALAR_POS = 32
 VECTOR_EXITS = 14
-SCALAR_LAYS = 0
 EXIT_UNITS, EXIT_COPIES = 5, 4
 GAP = 2
 
@@ -62,16 +61,14 @@ def tile_convnext_pointwise_pair_d7_kernel(
         g_ps = g_bank.tile([P, 4 * PASSES], F32, name="g_ps")
         w1s = sb([P, 16], F32, "w1s")
         w2s = sb([P, 64], F32, "w2s")
-        g_sb = sb([P, 4 * PASSES], BF16, "g_sb")
-        g32 = sb([P, 4 * PASSES], F32, "g32")
+        g_rows = sb([P, 512], BF16, "g_rows")
+        g_sb = sb([P, 4 * PASSES], F32, "g_sb")
         gamma_sb = sb([P, BLOCKS, 2], BF16, "gamma_sb")
         y_sb = [sb([P, 2, C], BF16, "y_sb%d" % j) for j in range(4)]
         y_laid = [sb([P, 1024], BF16, "y_laid%d" % j) for j in range(4)]
         y_codes = sb([P, NPOS], U32, "y_codes")
         y_scl = sb([P, NPOS], U8, "y_scl")
-        w1_first = [sb([P, 1024], U8, "w1_first%d" % h) for h in range(2)]
-        w1_raw = {k: sb([P, 2048], U8, "w1_raw%d" % k) for k in range(1, PASSES)}
-        w1_wide = [sb([P, 2048], BF16, "w1_wide%d" % k) for k in range(1)]
+        w1_raw = [sb([P, 2048], U8, "w1_raw%d" % k) for k in range(PASSES)]
         w1_laid = {k: sb([P, 2048], BF16, "w1_laid%d" % k) for k in (0, 1, 3)}
         w1_laid[2] = shared_tile([P, 2048])
         w1_codes = [sb([P, 512], U32, "w1_codes%d" % k) for k in range(PASSES)]
@@ -95,10 +92,6 @@ def tile_convnext_pointwise_pair_d7_kernel(
             src = w1_bytes.rearrange("(p t) n -> p t n", t=4)[:, :, 512 * k : 512 * (k + 1)]
             nc.sync.dma_start(out=w1_raw[k][:].rearrange("p (t n) -> p t n", t=4), in_=src)
 
-        def load_w1_half(h):
-            src = w1_bytes.rearrange("(p t) n -> p t n", t=4)[:, 2 * h : 2 * h + 2, 0:512]
-            nc.sync.dma_start(out=w1_first[h][:].rearrange("p (t n) -> p t n", t=2), in_=src)
-
         def load_y(j):
             nc.sync.dma_start(
                 out=y_sb[j][:], in_=y[256 * j : 256 * (j + 1), :].rearrange("(p a) k -> p a k", p=P)
@@ -111,14 +104,11 @@ def tile_convnext_pointwise_pair_d7_kernel(
             nc.scalar.copy(out=dst[:, lo:hi], in_=src[:, lo:hi].bitcast(FP8))
 
         def lay_w1(k, b):
-            dst = w1_laid[k][:].rearrange("p (s m t) -> p m t s", s=4, t=4)[:, 32 * b : 32 * (b + 1)]
-            src = (w1_wide[0][:] if k == 0 else w1_raw[k][:].bitcast(FP8)).rearrange("p (t m s) -> p m t s", t=4, s=4)[:, 32 * b : 32 * (b + 1)]
-            col = w1s[:, 4 * k + b : 4 * k + b + 1]
-            if 4 * k + b >= 16 - SCALAR_LAYS:
-                nc.scalar.activation(out=dst, in_=src, func=COPY, scale=col)
-            else:
-                dst, src = dst.rearrange("p m t s -> p m s t"), src.rearrange("p m t s -> p m s t")
-                nc.vector.tensor_scalar(out=dst, in0=src, scalar1=col, scalar2=None, op0=MULT)
+            dst = w1_laid[k][:].rearrange("p (s m t) -> p m s t", s=4, t=4)[:, 32 * b : 32 * (b + 1)]
+            src = w1_raw[k][:].bitcast(FP8).rearrange("p (t m s) -> p m s t", t=4, s=4)[:, 32 * b : 32 * (b + 1)]
+            nc.vector.tensor_scalar(
+                out=dst, in0=src, scalar1=w1s[:, 4 * k + b : 4 * k + b + 1], scalar2=None, op0=MULT
+            )
 
         def quantise(codes, scl, lo, hi, src):
             nc.vector.quantize_mx(out=codes[:, lo:hi].bitcast(FP8X4), scales=scl[:, lo:hi], in_=src)
@@ -219,7 +209,7 @@ def tile_convnext_pointwise_pair_d7_kernel(
                     out=h_laid[u - u % 2][:, u % 2, P - SCALAR_POS : P, t],
                     in_=gelus[u // 4][:, u % 4, P - SCALAR_POS : P, t],
                     func=COPY,
-                    scale=g32[:, col : col + 1],
+                    scale=g_sb[:, col : col + 1],
                 )
 
         def quantise_h(u, n):
@@ -264,18 +254,21 @@ def tile_convnext_pointwise_pair_d7_kernel(
             queue = nc.scalar if c == LAST and i % 2 else nc.sync
             queue.dma_start(out=out[P * i : P * (i + 1), cols], in_=o_sb[c][:, i, :])
 
+        zero = sb([P, 1], F32, "zero")
+        nc.vector.memset(zero[:], 0.0)
+        nc.vector.memset(g_rows[:], 0.0)
+
         for q in range(4):
             queue = nc.scalar if q % 2 else nc.sync
             queue.dma_start(out=w1s[32 * q : 32 * (q + 1), :], in_=w1_scale[q].partition_broadcast(32))
-        load_w1_half(0)
-        load_w1_half(1)
+        load_w1(0)
         load_w1(1)
         load_w1(2)
         load_y(0)
         make_identity(nc, ident[:])
-        load_w1(3)
+        nc.sync.dma_start(out=g_rows[0:PASSES, :], in_=g.rearrange("(k x) -> k x", k=PASSES))
         load_y(1)
-        nc.sync.dma_start(out=g_sb[:].rearrange("p (k t) -> p k t", t=4), in_=g.rearrange("(k p t) -> p k t", p=P, t=4))
+        load_w1(3)
         load_w2(0)
         w2_flat = w2_scale.rearrange("i j -> (i j)")
         for q in range(4):
@@ -288,29 +281,24 @@ def tile_convnext_pointwise_pair_d7_kernel(
         nc.sync.dma_start(out=r_sb[:], in_=r.rearrange("(i p) n -> p i n", p=P))
         nc.sync.dma_start(out=gamma_sb[:, :, 0:1], in_=gamma.rearrange("(i p) -> p i", p=P).unsqueeze(2))
 
-        zero = sb([P, 1], F32, "zero")
         warm = sb([P, 1], F32, "warm")
-        nc.vector.memset(zero[:], 0.0)
         nc.scalar.activation(out=warm[:], in_=zero[:], func=GELU)
         nc.vector.tensor_copy(out=ident16[:], in_=ident[:])
-        for h in range(2):
-            nc.scalar.copy(out=w1_wide[0][:, 1024 * h : 1024 * h + 512], in_=w1_first[h][:, 0:512].bitcast(FP8))
-            nc.vector.tensor_copy(
-                out=w1_wide[0][:, 1024 * h + 512 : 1024 * (h + 1)], in_=w1_first[h][:, 512:1024].bitcast(FP8)
-            )
         y_banks = [turn_y(0), turn_y(1)]
+        for t in range(4):
+            nc.tensor.matmul(g_ps[:, t::4], lhsT=g_rows[:, t::4], rhs=ident16[:, 0:PASSES], start=True, stop=True)
         exit_y(y_banks[0], 0)
         exit_y(y_banks[1], 1)
-        for n in range(16 - SCALAR_LAYS, 16):
-            lay_w1(*divmod(n, 4))
         widen_w2(0, 0)
         for n in range(0, 6):
             lay_w1(*divmod(n, 4))
         quantise_w1(0)
-        for n in range(6, 10):
+        for n in range(6, 9):
             lay_w1(*divmod(n, 4))
-        quantise_y(0)
         quantise_w1(1)
+        quantise_y(0)
+        for n in range(9, 12):
+            lay_w1(*divmod(n, 4))
         quantise_y(1)
 
         scalar_side = {u: [] for u in range(NUNITS)}
@@ -321,7 +309,7 @@ def tile_convnext_pointwise_pair_d7_kernel(
         def put(u, fn, *args):
             vector_side[u].append((fn, args))
 
-        scalar_side[SCALAR_UNITS[0] - GAP].append((nc.scalar.copy, (g32[:], g_sb[:])))
+        scalar_side[0].append((nc.scalar.copy, (g_sb[:], g_ps[:])))
         for u in SCALAR_UNITS:
             scalar_side[u | 1].append((scalar_gain, (u,)))
         for n in range(VECTOR_EXITS):
@@ -361,8 +349,7 @@ def tile_convnext_pointwise_pair_d7_kernel(
             steps.extend(bank_side[u])
         ahead = SCALAR_BANKS - 1
         filled = {j: steps[j][0](*steps[j][2]) for j in range(ahead)}
-        nc.tensor.matmul(g_ps[:], lhsT=ident16[:], rhs=g_sb[:], start=True, stop=True)
-        for n in range(10, 16 - SCALAR_LAYS):
+        for n in range(12, 16):
             lay_w1(*divmod(n, 4))
         quantise_w1(2)
         quantise_w1(3)

@@ -261,45 +261,36 @@ def tile_convnext_pointwise_pair_d7_kernel(
         for q in range(4):
             queue = nc.scalar if q % 2 else nc.sync
             queue.dma_start(out=w1s[32 * q : 32 * (q + 1), :], in_=w1_scale[q].partition_broadcast(32))
+        make_identity(nc, ident[:])
         load_w1(0)
         load_w1(1)
-        load_w1(2)
         load_y(0)
-        make_identity(nc, ident[:])
-        nc.sync.dma_start(out=g_rows[0:PASSES, :], in_=g.rearrange("(k x) -> k x", k=PASSES))
         load_y(1)
-        load_w1(3)
+        load_w1(2)
+        nc.sync.dma_start(out=g_rows[0:PASSES, :], in_=g.rearrange("(k x) -> k x", k=PASSES))
         load_w2(0)
+        load_w1(3)
         w2_flat = w2_scale.rearrange("i j -> (i j)")
         for q in range(4):
             nc.sync.dma_start(out=w2s[32 * q : 32 * (q + 1), 0:61], in_=w2_flat[q : q + 61].partition_broadcast(32))
-        load_y(2)
-        load_w2(1)
-        load_y(3)
-        load_w2(2)
-        load_w2(3)
+        for i in range(1, BLOCKS):
+            load_w2(i)
+            if i + 1 < 4:
+                load_y(i + 1)
         nc.sync.dma_start(out=r_sb[:], in_=r.rearrange("(i p) n -> p i n", p=P))
         nc.sync.dma_start(out=gamma_sb[:, :, 0:1], in_=gamma.rearrange("(i p) -> p i", p=P).unsqueeze(2))
 
         warm = sb([P, 1], F32, "warm")
         nc.scalar.activation(out=warm[:], in_=zero[:], func=GELU)
         nc.vector.tensor_copy(out=ident16[:], in_=ident[:])
-        y_banks = [turn_y(0), turn_y(1)]
-        for t in range(4):
-            nc.tensor.matmul(g_ps[:, t::4], lhsT=g_rows[:, t::4], rhs=ident16[:, 0:PASSES], start=True, stop=True)
-        exit_y(y_banks[0], 0)
-        exit_y(y_banks[1], 1)
-        widen_w2(0, 0)
-        for n in range(0, 6):
-            lay_w1(*divmod(n, 4))
-        quantise_w1(0)
-        for n in range(6, 9):
-            lay_w1(*divmod(n, 4))
-        quantise_w1(1)
-        quantise_y(0)
-        for n in range(9, 12):
-            lay_w1(*divmod(n, 4))
-        quantise_y(1)
+        for j in range(2):
+            exit_y(turn_y(j), j)
+        for k in range(2):
+            for b in range(4):
+                lay_w1(k, b)
+        for j in range(2):
+            quantise_w1(j)
+            quantise_y(j)
 
         scalar_side = {u: [] for u in range(NUNITS)}
         bank_side = {u: [] for u in range(NUNITS)}
@@ -309,7 +300,7 @@ def tile_convnext_pointwise_pair_d7_kernel(
         def put(u, fn, *args):
             vector_side[u].append((fn, args))
 
-        scalar_side[0].append((nc.scalar.copy, (g_sb[:], g_ps[:])))
+        scalar_side[1].append((nc.scalar.copy, (g_sb[:], g_ps[:])))
         for u in SCALAR_UNITS:
             scalar_side[u | 1].append((scalar_gain, (u,)))
         for n in range(VECTOR_EXITS):
@@ -317,14 +308,14 @@ def tile_convnext_pointwise_pair_d7_kernel(
             u = EXIT_UNITS * n // EXIT_COPIES + 1
             if k % 2 == 0:
                 if n:
-                    scalar_side[u - GAP].append((widen_w2, (i, k // 2)))
+                    scalar_side[u - 1 - GAP].append((widen_w2, (i, k // 2)))
                 put(u - 1, turn_w2, i, k // 2)
             put(u, exit_w2, i, k)
             if k == PASSES - 1:
                 runs[4 * (u // 4) + 4].append((quantise_w2, (i,)))
         for j in (2, 3):
-            bank_side[8 * j - 12 - GAP].append((turn_y, exit_y, (j,)))
-            runs[8 * j - 12].append((quantise_y, (j,)))
+            bank_side[4 * (j + 1) - GAP].append((turn_y, exit_y, (j,)))
+            runs[4 * (j + 1)][:0] = [(quantise_y, (j,))]
         banks = [(c, range(i, i + 4 // nb)) for c, (b0, nb) in enumerate(CHUNKS[:LAST]) for i in range(0, BLOCKS, 4 // nb)]
         first = PASSES * CHUNKS[0][1]
         for n, (c, blocks) in enumerate(banks):
@@ -349,8 +340,12 @@ def tile_convnext_pointwise_pair_d7_kernel(
             steps.extend(bank_side[u])
         ahead = SCALAR_BANKS - 1
         filled = {j: steps[j][0](*steps[j][2]) for j in range(ahead)}
-        for n in range(12, 16):
-            lay_w1(*divmod(n, 4))
+        for t in range(4):
+            nc.tensor.matmul(g_ps[:, t::4], lhsT=g_rows[:, t::4], rhs=ident16[:, 0:PASSES], start=True, stop=True)
+        widen_w2(0, 0)
+        for k in range(2, PASSES):
+            for b in range(4):
+                lay_w1(k, b)
         quantise_w1(2)
         quantise_w1(3)
 
@@ -364,10 +359,10 @@ def tile_convnext_pointwise_pair_d7_kernel(
             for fn, fn_args in scalar_side[u]:
                 fn(*fn_args)
             if u in runs:
-                for fn, fn_args in runs[u]:
+                own, shared = (quantise_h, (u - 2, 2)), (quantise_h, (u - 4, 2))
+                calls = runs[u][:-1] + [own, shared] + runs[u][-1:] if runs[u] else [shared, own]
+                for fn, fn_args in calls:
                     fn(*fn_args)
-                quantise_h(u - 4, 2)
-                quantise_h(u - 2, 2)
             gain(u)
             for fn, fn_args in vector_side[u]:
                 fn(*fn_args)

@@ -28,10 +28,11 @@ NUNITS = len(UNITS)
 SCALAR_BANKS = 4
 VECTOR_BANKS = 3
 
-POOL_POS = 100
-POOL_POS_LAST = 56
-SCALAR_UNITS = (NUNITS - 10, NUNITS - 6, NUNITS - 2, NUNITS - 1)
+POOL_POS = 200
+POOL_POS_LAST = 120
+SCALAR_UNITS = (NUNITS - 13, NUNITS - 9, NUNITS - 5, NUNITS - 2, NUNITS - 1)
 SCALAR_POS = 32
+SCALAR_LAYS = 2
 VECTOR_EXITS = 14
 EXIT_UNITS, EXIT_COPIES = 5, 4
 GAP = 2
@@ -43,7 +44,7 @@ def tile_convnext_pointwise_pair_d7_kernel(
     nc = tc.nc
     with ExitStack() as ctx:
         keep = ctx.enter_context(tc.tile_pool(name="keep", bufs=1))
-        gelu_pool = ctx.enter_context(tc.tile_pool(name="gelu_pool", bufs=3))
+        gelu_pool = ctx.enter_context(tc.tile_pool(name="gelu_pool", bufs=4))
         h_pool = ctx.enter_context(tc.tile_pool(name="h_pool", bufs=2))
         scalar_banks = ctx.enter_context(tc.psum_pool(name="scalar_banks", bufs=SCALAR_BANKS))
         vector_banks = ctx.enter_context(tc.psum_pool(name="vector_banks", bufs=VECTOR_BANKS))
@@ -69,6 +70,7 @@ def tile_convnext_pointwise_pair_d7_kernel(
         y_codes = sb([P, NPOS], U32, "y_codes")
         y_scl = sb([P, NPOS], U8, "y_scl")
         w1_raw = [sb([P, 2048], U8, "w1_raw%d" % k) for k in range(PASSES)]
+        w1_wide = sb([P, 4, P * SCALAR_LAYS], BF16, "w1_wide")
         w1_laid = {k: sb([P, 2048], BF16, "w1_laid%d" % k) for k in (0, 1, 3)}
         w1_laid[2] = shared_tile([P, 2048])
         w1_codes = [sb([P, 512], U32, "w1_codes%d" % k) for k in range(PASSES)]
@@ -109,6 +111,12 @@ def tile_convnext_pointwise_pair_d7_kernel(
             nc.vector.tensor_scalar(
                 out=dst, in0=src, scalar1=w1s[:, 4 * k + b : 4 * k + b + 1], scalar2=None, op0=MULT
             )
+
+        def lay_w1_scalar(n):
+            b = 4 - SCALAR_LAYS + n
+            dst = w1_laid[1][:].rearrange("p (s m t) -> p m t s", s=4, t=4)[:, 32 * b : 32 * (b + 1)]
+            src = w1_wide[:].rearrange("p t (m s) -> p m t s", s=4)[:, 32 * n : 32 * (n + 1)]
+            nc.scalar.activation(out=dst, in_=src, func=COPY, scale=w1s[:, 4 + b : 5 + b])
 
         def quantise(codes, scl, lo, hi, src):
             nc.vector.quantize_mx(out=codes[:, lo:hi].bitcast(FP8X4), scales=scl[:, lo:hi], in_=src)
@@ -177,30 +185,33 @@ def tile_convnext_pointwise_pair_d7_kernel(
                 gelus[u // 4] = gelu_pool.tile([P, 4, P, 4], F32, name="gelus")
             nc.scalar.activation(out=gelus[u // 4][:, u % 4], in_=z[:].rearrange("p s n -> p n s"), func=GELU)
 
-        def gain_part(eng, g_tile, dst, u, n, lo, hi):
+        def gain_part(eng, g_tile, u, n, lo, hi):
             k0, k1 = UNITS[u][0], UNITS[u + n - 1][0]
+            m = k1 - k0 + 1
+            cols = slice(lo // m, hi // m)
+            dst = h_laid[u - u % 2][:, u % 2 : u % 2 + n].rearrange("p (m u) n t -> p m (u n) t", m=m)
+            src = gelus[u // 4][:, u % 4 : u % 4 + n].rearrange("p (m u) n t -> p m (u n) t", m=m)
             g_part = g_tile[:, 4 * k0 : 4 * (k1 + 1)].rearrange("p (k t) -> p k t", t=4)
             eng.tensor_tensor(
-                out=dst[:, :, lo:hi],
-                in0=gelus[u // 4][:, u % 4 : u % 4 + n, lo:hi],
-                in1=g_part.unsqueeze(2).to_broadcast([P, n, hi - lo, 4]),
+                out=dst[:, :, cols],
+                in0=src[:, :, cols],
+                in1=g_part.unsqueeze(2).to_broadcast([P, m, (hi - lo) // m, 4]),
                 op=MULT,
             )
 
         def gain(u):
-            first_unit = u - u % 4
-            last_group = first_unit == NUNITS - 4
-            cut = POOL_POS_LAST if last_group else POOL_POS
+            cut = POOL_POS_LAST if u // 4 == NUNITS // 4 - 1 else POOL_POS
+            left = SCALAR_POS if u in SCALAR_UNITS else 0
             if u % 4 == 1:
-                h_laid[first_unit] = shared_tile([P, 2, P, 4])
-                gain_part(nc.gpsimd, g_sb, h_laid[first_unit], first_unit, 2, 0, cut)
+                h_laid[u - 1] = shared_tile([P, 2, P, 4])
+                gain_part(nc.gpsimd, g_sb, u - 1, 2, 0, cut)
+                gain_part(nc.vector, g_ps, u - 1, 2, cut, 2 * P)
             if u % 4 == 2:
                 h_laid[u] = h_pool.tile([P, 2, P, 4], BF16, name="vector_h", align_bytes=64)
-            if u % 4 > 1:
-                hi = P - SCALAR_POS if u in SCALAR_UNITS else P
-                gain_part(nc.vector, g_ps, h_laid[u - u % 2][:, u % 2 : u % 2 + 1], u, 1, 0, hi)
-            if u % 4 == (1 if last_group else 2):
-                gain_part(nc.vector, g_ps, h_laid[first_unit], first_unit, 2, cut, P)
+            if u % 4 > 1 and UNITS[u - u % 2][0] != UNITS[u | 1][0]:
+                gain_part(nc.vector, g_ps, u, 1, 0, P - left)
+            elif u % 4 == 3:
+                gain_part(nc.vector, g_ps, u - 1, 2, 0, 2 * P - left)
 
         def scalar_gain(u):
             for t in range(4):
@@ -265,10 +276,10 @@ def tile_convnext_pointwise_pair_d7_kernel(
         load_w1(0)
         load_w1(1)
         load_y(0)
-        load_y(1)
         load_w1(2)
-        nc.sync.dma_start(out=g_rows[0:PASSES, :], in_=g.rearrange("(k x) -> k x", k=PASSES))
+        load_y(1)
         load_w2(0)
+        nc.sync.dma_start(out=g_rows[0:PASSES, :], in_=g.rearrange("(k x) -> k x", k=PASSES))
         load_w1(3)
         w2_flat = w2_scale.rearrange("i j -> (i j)")
         for q in range(4):
@@ -283,14 +294,22 @@ def tile_convnext_pointwise_pair_d7_kernel(
         warm = sb([P, 1], F32, "warm")
         nc.scalar.activation(out=warm[:], in_=zero[:], func=GELU)
         nc.vector.tensor_copy(out=ident16[:], in_=ident[:])
-        for j in range(2):
-            exit_y(turn_y(j), j)
-        for k in range(2):
-            for b in range(4):
-                lay_w1(k, b)
-        for j in range(2):
-            quantise_w1(j)
-            quantise_y(j)
+        y_banks = [turn_y(0), turn_y(1)]
+        src = w1_raw[1][:].bitcast(FP8).rearrange("p (t n) -> p t n", t=4)
+        nc.scalar.copy(out=w1_wide[:], in_=src[:, :, 512 - P * SCALAR_LAYS :])
+        for n in range(SCALAR_LAYS):
+            lay_w1_scalar(n)
+            exit_y(y_banks[n], n)
+        lays = [(k, b) for k in range(PASSES) for b in range(4 - SCALAR_LAYS if k == 1 else 4)]
+        for args in lays[:6]:
+            lay_w1(*args)
+        quantise_w1(0)
+        for args in lays[6:8]:
+            lay_w1(*args)
+        quantise_y(0)
+        lay_w1(*lays[8])
+        quantise_w1(1)
+        quantise_y(1)
 
         scalar_side = {u: [] for u in range(NUNITS)}
         bank_side = {u: [] for u in range(NUNITS)}
@@ -343,9 +362,8 @@ def tile_convnext_pointwise_pair_d7_kernel(
         for t in range(4):
             nc.tensor.matmul(g_ps[:, t::4], lhsT=g_rows[:, t::4], rhs=ident16[:, 0:PASSES], start=True, stop=True)
         widen_w2(0, 0)
-        for k in range(2, PASSES):
-            for b in range(4):
-                lay_w1(k, b)
+        for args in lays[9:]:
+            lay_w1(*args)
         quantise_w1(2)
         quantise_w1(3)
 

from contextlib import ExitStack

import concourse.mybir as mybir
from concourse.masks import make_identity

F32 = mybir.dt.float32
BF16 = mybir.dt.bfloat16
U32 = mybir.dt.uint32
U8 = mybir.dt.uint8
FP8 = mybir.dt.float8_e4m3fn
FP8X4 = mybir.dt.float8_e4m3fn_x4
MULT = mybir.AluOpType.mult
ADD = mybir.AluOpType.add
GELU = mybir.ActivationFunctionType.Gelu_apprx_tanh
COPY = mybir.ActivationFunctionType.Copy

P = 128
NPOS, C, H = 1024, 512, 2048
PASSES = H // 512
BLOCKS = C // P
FLOPS = 2 * NPOS * C * H * 2

CHUNKS = ((0, 4), (4, 2), (6, 1), (7, 1))
LAST = len(CHUNKS) - 1
UNITS = [(k, b0 + b) for b0, nb in CHUNKS for k in range(PASSES) for b in range(nb)]
NUNITS = len(UNITS)

SCALAR_BANKS = 4
VECTOR_BANKS = 3

POOL_POS = 200
POOL_POS_LAST = 120
SCALAR_UNITS = (NUNITS - 13, NUNITS - 9, NUNITS - 5, NUNITS - 2, NUNITS - 1)
SCALAR_POS = 32
SCALAR_LAYS = 2
VECTOR_EXITS = 14
EXIT_UNITS, EXIT_COPIES = 5, 4
GAP = 2


def tile_convnext_pointwise_pair_d7_kernel(
    tc, y, w1_bytes, w1_scale, g, w2_bytes, w2_scale, gamma, r, out
):
    nc = tc.nc
    with ExitStack() as ctx:
        keep = ctx.enter_context(tc.tile_pool(name="keep", bufs=1))
        gelu_pool = ctx.enter_context(tc.tile_pool(name="gelu_pool", bufs=4))
        h_pool = ctx.enter_context(tc.tile_pool(name="h_pool", bufs=2))
        scalar_banks = ctx.enter_context(tc.psum_pool(name="scalar_banks", bufs=SCALAR_BANKS))
        vector_banks = ctx.enter_context(tc.psum_pool(name="vector_banks", bufs=VECTOR_BANKS))
        g_bank = ctx.enter_context(tc.psum_pool(name="g_bank", bufs=1))
        ctx.enter_context(tc.manual_schedule())

        def sb(shape, dt, name):
            return keep.tile(shape, dt, name=name, align_bytes=64)

        def shared_tile(shape):
            return h_pool.tile(shape, BF16, name="shared", bufs=1, align_bytes=64)

        ident = sb([P, P], F32, "ident")
        ident16 = sb([P, P], BF16, "ident16")
        g_ps = g_bank.tile([P, 4 * PASSES], F32, name="g_ps")
        w1s = sb([P, 16], F32, "w1s")
        w2s = sb([P, 64], F32, "w2s")
        g_rows = sb([P, 512], BF16, "g_rows")
        g_sb = sb([P, 4 * PASSES], F32, "g_sb")
        gamma_sb = sb([P, BLOCKS, 2], BF16, "gamma_sb")
        y_sb = [sb([P, 2, C], BF16, "y_sb%d" % j) for j in range(4)]
        y_laid = [sb([P, 1024], BF16, "y_laid%d" % j) for j in range(4)]
        y_codes = sb([P, NPOS], U32, "y_codes")
        y_scl = sb([P, NPOS], U8, "y_scl")
        w1_raw = [sb([P, 2048], U8, "w1_raw%d" % k) for k in range(PASSES)]
        w1_wide = sb([P, 4, P * SCALAR_LAYS], BF16, "w1_wide")
        w1_laid = {k: sb([P, 2048], BF16, "w1_laid%d" % k) for k in (0, 1, 3)}
        w1_laid[2] = shared_tile([P, 2048])
        w1_codes = [sb([P, 512], U32, "w1_codes%d" % k) for k in range(PASSES)]
        w1_scl = [sb([P, 512], U8, "w1_scl%d" % k) for k in range(PASSES)]
        w2_raw = [sb([P, 2048], U8, "w2_raw%d" % i) for i in range(BLOCKS)]
        w2_wide = [sb([P, 2048], BF16, "w2_wide%d" % i) for i in range(BLOCKS)]
        w2_laid = [sb([P, 2048], BF16, "w2_laid%d" % i) for i in range(BLOCKS)]
        w2_codes = [sb([P, 512], U32, "w2_codes%d" % i) for i in range(BLOCKS)]
        w2_scl = [sb([P, 512], U8, "w2_scl%d" % i) for i in range(BLOCKS)]
        h_codes = [sb([P, 512], U32, "h_codes%d" % q) for q in range(NUNITS // 4)]
        h_scl = [sb([P, 512], U8, "h_scl%d" % q) for q in range(NUNITS // 4)]
        r_sb = sb([P, BLOCKS, NPOS], BF16, "r_sb")
        o_sb = [sb([P, BLOCKS, P * nb], F32, "o_sb%d" % c) for c, (b0, nb) in enumerate(CHUNKS)]

        gelus = {}
        h_laid = {}
        w2_turned = {}
        acc = {}

        def load_w1(k):
            src = w1_bytes.rearrange("(p t) n -> p t n", t=4)[:, :, 512 * k : 512 * (k + 1)]
            nc.sync.dma_start(out=w1_raw[k][:].rearrange("p (t n) -> p t n", t=4), in_=src)

        def load_y(j):
            nc.sync.dma_start(
                out=y_sb[j][:], in_=y[256 * j : 256 * (j + 1), :].rearrange("(p a) k -> p a k", p=P)
            )

        def load_w2(i):
            nc.sync.dma_start(out=w2_raw[i][:], in_=w2_bytes[P * i : P * (i + 1), :])

        def widen(dst, src, lo, hi):
            nc.scalar.copy(out=dst[:, lo:hi], in_=src[:, lo:hi].bitcast(FP8))

        def lay_w1(k, b):
            dst = w1_laid[k][:].rearrange("p (s m t) -> p m s t", s=4, t=4)[:, 32 * b : 32 * (b + 1)]
            src = w1_raw[k][:].bitcast(FP8).rearrange("p (t m s) -> p m s t", t=4, s=4)[:, 32 * b : 32 * (b + 1)]
            nc.vector.tensor_scalar(
                out=dst, in0=src, scalar1=w1s[:, 4 * k + b : 4 * k + b + 1], scalar2=None, op0=MULT
            )

        def lay_w1_scalar(n):
            b = 4 - SCALAR_LAYS + n
            dst = w1_laid[1][:].rearrange("p (s m t) -> p m t s", s=4, t=4)[:, 32 * b : 32 * (b + 1)]
            src = w1_wide[:].rearrange("p t (m s) -> p m t s", s=4)[:, 32 * n : 32 * (n + 1)]
            nc.scalar.activation(out=dst, in_=src, func=COPY, scale=w1s[:, 4 + b : 5 + b])

        def quantise(codes, scl, lo, hi, src):
            nc.vector.quantize_mx(out=codes[:, lo:hi].bitcast(FP8X4), scales=scl[:, lo:hi], in_=src)

        def quantise_w1(k):
            quantise(w1_codes[k], w1_scl[k], 0, 512, w1_laid[k][:])

        def quantise_w2(i):
            quantise(w2_codes[i], w2_scl[i], 0, 512, w2_laid[i][:])

        def quantise_y(j):
            quantise(y_codes, y_scl, 256 * j, 256 * (j + 1), y_laid[j][:])

        def turn(pool, words):
            bank = pool.tile([P, 2, 2, P], F32, name="bank")
            for a in range(2):
                for u in range(2):
                    nc.tensor.transpose(bank[:, a, u, :], words[:, 256 * a + u : 256 * (a + 1) : 2], ident[:])
            return bank

        def turn_y(j):
            return turn(scalar_banks, y_sb[j][:].rearrange("p a k -> p (a k)").bitcast(F32))

        def exit_y(bank, j):
            dst = y_laid[j][:].bitcast(F32).rearrange("p (n a u) -> p n a u", a=2, u=2)
            nc.scalar.copy(out=dst, in_=bank[:].rearrange("p a u n -> p n a u"))

        def widen_w2(i, half):
            widen(w2_wide[i], w2_raw[i], 1024 * half, 1024 * (half + 1))

        def turn_w2(i, half):
            pool = vector_banks if PASSES * i + 2 * half < VECTOR_EXITS else scalar_banks
            w2_turned[i, half] = turn(pool, w2_wide[i][:, 1024 * half : 1024 * (half + 1)].bitcast(F32))

        def exit_w2(i, k):
            dst = w2_laid[i][:, 512 * k : 512 * (k + 1)].rearrange("p (n u e) -> p n u e", u=2, e=2)
            src = w2_turned[i, k // 2][:, k % 2].rearrange("p u n -> p (u n)").bitcast(BF16)
            src = src.rearrange("p (u n e) -> p n u e", u=2, e=2)
            col = w2s[:, 16 * i + 4 * k : 16 * i + 4 * k + 1]
            if PASSES * i + k < VECTOR_EXITS:
                nc.vector.tensor_scalar(out=dst, in0=src, scalar1=col, scalar2=None, op0=MULT)
            else:
                nc.scalar.activation(out=dst, in_=src, func=COPY, scale=col)

        def exit_w2_bank(bank, i, half):
            exit_w2(i, 2 * half)
            exit_w2(i, 2 * half + 1)

        def expand(u):
            k, b = UNITS[u]
            z = scalar_banks.tile([P, 4, P], F32, name="bank")
            for s in range(4):
                nc.tensor.matmul_mx(
                    out=z[:, s, :],
                    lhsT=w1_codes[k][:, P * s : P * (s + 1)].bitcast(FP8X4),
                    lhsT_scale=w1_scl[k][:, P * s : P * (s + 1)],
                    rhs=y_codes[:, P * b : P * (b + 1)].bitcast(FP8X4),
                    rhs_scale=y_scl[:, P * b : P * (b + 1)],
                    start=True,
                    stop=True,
                )
            return z

        def gelu(z, u):
            if u % 4 == 0:
                gelus[u // 4] = gelu_pool.tile([P, 4, P, 4], F32, name="gelus")
            nc.scalar.activation(out=gelus[u // 4][:, u % 4], in_=z[:].rearrange("p s n -> p n s"), func=GELU)

        def gain_part(eng, g_tile, u, n, lo, hi):
            k0, k1 = UNITS[u][0], UNITS[u + n - 1][0]
            m = k1 - k0 + 1
            cols = slice(lo // m, hi // m)
            dst = h_laid[u - u % 2][:, u % 2 : u % 2 + n].rearrange("p (m u) n t -> p m (u n) t", m=m)
            src = gelus[u // 4][:, u % 4 : u % 4 + n].rearrange("p (m u) n t -> p m (u n) t", m=m)
            g_part = g_tile[:, 4 * k0 : 4 * (k1 + 1)].rearrange("p (k t) -> p k t", t=4)
            eng.tensor_tensor(
                out=dst[:, :, cols],
                in0=src[:, :, cols],
                in1=g_part.unsqueeze(2).to_broadcast([P, m, (hi - lo) // m, 4]),
                op=MULT,
            )

        def gain(u):
            cut = POOL_POS_LAST if u // 4 == NUNITS // 4 - 1 else POOL_POS
            left = SCALAR_POS if u in SCALAR_UNITS else 0
            if u % 4 == 1:
                h_laid[u - 1] = shared_tile([P, 2, P, 4])
                gain_part(nc.gpsimd, g_sb, u - 1, 2, 0, cut)
                gain_part(nc.vector, g_ps, u - 1, 2, cut, 2 * P)
            if u % 4 == 2:
                h_laid[u] = h_pool.tile([P, 2, P, 4], BF16, name="vector_h", align_bytes=64)
            if u % 4 > 1 and UNITS[u - u % 2][0] != UNITS[u | 1][0]:
                gain_part(nc.vector, g_ps, u, 1, 0, P - left)
            elif u % 4 == 3:
                gain_part(nc.vector, g_ps, u - 1, 2, 0, 2 * P - left)

        def scalar_gain(u):
            for t in range(4):
                col = 4 * UNITS[u][0] + t
                nc.scalar.activation(
                    out=h_laid[u - u % 2][:, u % 2, P - SCALAR_POS : P, t],
                    in_=gelus[u // 4][:, u % 4, P - SCALAR_POS : P, t],
                    func=COPY,
                    scale=g_sb[:, col : col + 1],
                )

        def quantise_h(u, n):
            src = h_laid[u - u % 2][:, u % 2 : u % 2 + n].rearrange("p u n t -> p (u n t)")
            quantise(h_codes[u // 4], h_scl[u // 4], P * (u % 4), P * (u % 4 + n), src)

        def open_sums(pool, c, blocks):
            bank = pool.tile([P, len(blocks), P * CHUNKS[c][1]], F32, name="bank")
            for n, i in enumerate(blocks):
                acc[c, i] = bank[:, n, :]

        def contract(c, i, k, start, stop):
            b0, nb = CHUNKS[c]
            u = UNITS.index((k, b0))
            cols = slice(P * (u % 4), P * (u % 4 + nb))
            nc.tensor.matmul_mx(
                out=acc[c, i],
                lhsT=w2_codes[i][:, P * k : P * (k + 1)].bitcast(FP8X4),
                lhsT_scale=w2_scl[i][:, P * k : P * (k + 1)],
                rhs=h_codes[u // 4][:, cols].bitcast(FP8X4),
                rhs_scale=h_scl[u // 4][:, cols],
                start=start,
                stop=stop,
            )

        def contract_bank(c, blocks):
            open_sums(vector_banks, c, blocks)
            for i in blocks:
                for k in range(PASSES):
                    contract(c, i, k, k == 0, k == PASSES - 1)

        def contract_last(k):
            for i in range(BLOCKS):
                contract(LAST, i, k, k == 0 and i % 2 == 0, k == PASSES - 1 and i % 2 == 1)

        def finish(c, i):
            b0, nb = CHUNKS[c]
            cols = slice(P * b0, P * (b0 + nb))
            nc.vector.scalar_tensor_tensor(
                out=o_sb[c][:, i, :], in0=acc[c, i], scalar=gamma_sb[:, i, 0:1], in1=r_sb[:, i, cols], op0=MULT, op1=ADD
            )
            queue = nc.scalar if c == LAST and i % 2 else nc.sync
            queue.dma_start(out=out[P * i : P * (i + 1), cols], in_=o_sb[c][:, i, :])

        zero = sb([P, 1], F32, "zero")
        nc.vector.memset(zero[:], 0.0)
        nc.vector.memset(g_rows[:], 0.0)

        for q in range(4):
            queue = nc.scalar if q % 2 else nc.sync
            queue.dma_start(out=w1s[32 * q : 32 * (q + 1), :], in_=w1_scale[q].partition_broadcast(32))
        make_identity(nc, ident[:])
        load_w1(0)
        load_w1(1)
        load_y(0)
        load_w1(2)
        load_y(1)
        load_w2(0)
        nc.sync.dma_start(out=g_rows[0:PASSES, :], in_=g.rearrange("(k x) -> k x", k=PASSES))
        load_w1(3)
        w2_flat = w2_scale.rearrange("i j -> (i j)")
        for q in range(4):
            nc.sync.dma_start(out=w2s[32 * q : 32 * (q + 1), 0:61], in_=w2_flat[q : q + 61].partition_broadcast(32))
        for i in range(1, BLOCKS):
            load_w2(i)
            if i + 1 < 4:
                load_y(i + 1)
        nc.sync.dma_start(out=r_sb[:], in_=r.rearrange("(i p) n -> p i n", p=P))
        nc.sync.dma_start(out=gamma_sb[:, :, 0:1], in_=gamma.rearrange("(i p) -> p i", p=P).unsqueeze(2))

        warm = sb([P, 1], F32, "warm")
        nc.scalar.activation(out=warm[:], in_=zero[:], func=GELU)
        nc.vector.tensor_copy(out=ident16[:], in_=ident[:])
        y_banks = [turn_y(0), turn_y(1)]
        src = w1_raw[1][:].bitcast(FP8).rearrange("p (t n) -> p t n", t=4)
        nc.scalar.copy(out=w1_wide[:], in_=src[:, :, 512 - P * SCALAR_LAYS :])
        for n in range(SCALAR_LAYS):
            lay_w1_scalar(n)
            exit_y(y_banks[n], n)
        lays = [(k, b) for k in range(PASSES) for b in range(4 - SCALAR_LAYS if k == 1 else 4)]
        for args in lays[:6]:
            lay_w1(*args)
        quantise_w1(0)
        for args in lays[6:8]:
            lay_w1(*args)
        quantise_y(0)
        lay_w1(*lays[8])
        quantise_w1(1)
        quantise_y(1)

        scalar_side = {u: [] for u in range(NUNITS)}
        bank_side = {u: [] for u in range(NUNITS)}
        vector_side = {u: [] for u in range(NUNITS)}
        runs = {u: [] for u in range(4, NUNITS, 4)}

        def put(u, fn, *args):
            vector_side[u].append((fn, args))

        scalar_side[1].append((nc.scalar.copy, (g_sb[:], g_ps[:])))
        for u in SCALAR_UNITS:
            scalar_side[u | 1].append((scalar_gain, (u,)))
        for n in range(VECTOR_EXITS):
            i, k = divmod(n, PASSES)
            u = EXIT_UNITS * n // EXIT_COPIES + 1
            if k % 2 == 0:
                if n:
                    scalar_side[u - 1 - GAP].append((widen_w2, (i, k // 2)))
                put(u - 1, turn_w2, i, k // 2)
            put(u, exit_w2, i, k)
            if k == PASSES - 1:
                runs[4 * (u // 4) + 4].append((quantise_w2, (i,)))
        for j in (2, 3):
            bank_side[4 * (j + 1) - GAP].append((turn_y, exit_y, (j,)))
            runs[4 * (j + 1)][:0] = [(quantise_y, (j,))]
        banks = [(c, range(i, i + 4 // nb)) for c, (b0, nb) in enumerate(CHUNKS[:LAST]) for i in range(0, BLOCKS, 4 // nb)]
        first = PASSES * CHUNKS[0][1]
        for n, (c, blocks) in enumerate(banks):
            u = first + 2 * n + 1
            put(u, contract_bank, c, blocks)
            if c < LAST - 1:
                for i in blocks:
                    put(u + GAP, finish, c, i)
        u = first + 4 - GAP
        scalar_side[u - (SCALAR_BANKS - 1) - GAP].append((widen_w2, (BLOCKS - 1, 1)))
        bank_side[u].append((turn_w2, exit_w2_bank, (BLOCKS - 1, 1)))
        runs[first + 4].append((quantise_w2, (BLOCKS - 1,)))
        put(NUNITS - 2, quantise_h, NUNITS - 4, 2)
        for pair in range(2):
            put(NUNITS - 2, open_sums, scalar_banks, LAST, [2 * pair, 2 * pair + 1])
        put(NUNITS - 2, contract_last, 0)
        put(NUNITS - 2, contract_last, 1)

        steps = []
        for u in range(NUNITS):
            steps.append((expand, gelu, (u,)))
            steps.extend(bank_side[u])
        ahead = SCALAR_BANKS - 1
        filled = {j: steps[j][0](*steps[j][2]) for j in range(ahead)}
        for t in range(4):
            nc.tensor.matmul(g_ps[:, t::4], lhsT=g_rows[:, t::4], rhs=ident16[:, 0:PASSES], start=True, stop=True)
        widen_w2(0, 0)
        for args in lays[9:]:
            lay_w1(*args)
        quantise_w1(2)
        quantise_w1(3)

        for j, (fill, empty, args) in enumerate(steps):
            if j + ahead < len(steps):
                filled[j + ahead] = steps[j + ahead][0](*steps[j + ahead][2])
            empty(filled[j], *args)
            if fill is not expand:
                continue
            u = args[0]
            for fn, fn_args in scalar_side[u]:
                fn(*fn_args)
            if u in runs:
                own, shared = (quantise_h, (u - 2, 2)), (quantise_h, (u - 4, 2))
                calls = runs[u][:-1] + [own, shared] + runs[u][-1:] if runs[u] else [shared, own]
                for fn, fn_args in calls:
                    fn(*fn_args)
            gain(u)
            for fn, fn_args in vector_side[u]:
                fn(*fn_args)

        quantise_h(NUNITS - 2, 1)
        contract_last(PASSES - 2)
        finish(LAST - 1, 0)
        quantise_h(NUNITS - 1, 1)
        contract_last(PASSES - 1)
        for i in range(1, BLOCKS):
            finish(LAST - 1, i)
        for i in range(BLOCKS):
            finish(LAST, i)
